import numpy as np
import ml_dtypes


def mxq(x, axis, fmt="e4m3"):
    dtype, down = {"e4m3": (ml_dtypes.float8_e4m3fn, 7), "e5m2": (ml_dtypes.float8_e5m2, 14)}[fmt]
    v = np.moveaxis(np.asarray(x, np.float32).astype(ml_dtypes.bfloat16).astype(np.float64), axis, -1)
    blocks = v.reshape(v.shape[:-1] + (-1, 32))
    amax = np.abs(blocks).max(-1, keepdims=True)
    byte = np.maximum(np.where(amax > 0, np.frexp(amax)[1] - 1 + 127, 0) - down, 1)
    scale = np.exp2(byte - 127.0)
    codes = (blocks / scale).astype(np.float32).astype(dtype).astype(np.float64)
    return np.moveaxis((codes * scale).reshape(v.shape), -1, axis)


WIDE = False


def mx_kscale(k):
    if not WIDE:
        return np.ones(k)
    levels = np.array([10, -10, 5, -5, 0])
    if k % 512:
        return np.exp2(np.random.permutation(np.resize(levels, k // 32))).repeat(32)
    a = np.empty((k // 512, 16))
    for p in range(k // 512):
        a[p, :8] = np.random.permutation(np.resize(levels, 8))
        for g in range(8):
            far = levels[np.abs(levels - a[p, g]) >= 10]
            a[p, g + 8] = far[np.random.randint(len(far))]
    return np.exp2(a.ravel()).repeat(32)


def f64(x):
    return np.asarray(x).astype(np.float64)


def striped(idx):
    return np.tile(idx.reshape(-1, 16).T, (8, 1)).astype(np.uint16)


def unstriped(offs):
    return offs[:16].T.reshape(-1).astype(np.int64)


E2M1 = np.array([0.0, 0.5, 1.0, 1.5, 2.0, 3.0, 4.0, 6.0, -0.0, -0.5, -1.0, -1.5, -2.0, -3.0, -4.0, -6.0])


def pack_weight(w, fmt):
    k, n = w.shape
    w = f64(np.asarray(w, np.float32).astype(ml_dtypes.bfloat16)).reshape(k // 32, 32, n)
    amax = np.abs(w).max(1)
    if fmt == "e4m3":
        byte = np.frexp(amax)[1] - 1 + 127 - 7
    else:
        mant, ex = np.frexp(amax / 6.0)
        byte = np.where(mant > 0.5, ex, ex - 1) + 127
    byte = np.clip(np.where(amax > 0, byte, 1), 1, 254)
    scaled = (w * np.exp2(127.0 - byte)[:, None, :]).reshape(k, n).astype(np.float32)
    by_word = np.ascontiguousarray(scaled.reshape(k // 512, 128, 4, n).transpose(0, 1, 3, 2))
    if fmt == "e4m3":
        words = by_word.astype(ml_dtypes.float8_e4m3fn).view(np.uint8)
    else:
        c = by_word.astype(ml_dtypes.float4_e2m1fn).view(np.uint8) & 0xF
        words = (c[..., 0::2] | (c[..., 1::2] << 4)).reshape(k // 512, 128, 2 * n)
    return np.ascontiguousarray(words), np.ascontiguousarray(byte.astype(np.uint8).reshape(k // 512, 16, n))


def unpack_weight(words, scales, fmt):
    g, _, n = scales.shape
    words = np.ascontiguousarray(words).reshape(g, 128, n, -1)
    if fmt == "e4m3":
        vals = words.view(ml_dtypes.float8_e4m3fn).astype(np.float64)
    else:
        nib = np.empty((g, 128, n, 4), np.uint8)
        nib[..., 0::2] = words & 0xF
        nib[..., 1::2] = words >> 4
        vals = E2M1[nib]
    vals = vals * np.repeat(np.exp2(scales.astype(np.float64) - 127.0), 8, axis=1)[..., None]
    return vals.transpose(0, 1, 3, 2).reshape(g * 512, n)


def gelu(v):
    return 0.5 * v * (1.0 + np.tanh(np.sqrt(2.0 / np.pi) * (v + 0.044715 * v**3)))


def pack_table4(v):
    words, scales = pack_weight(v, "e2m1")
    g, t = words.shape[0] // 2, v.shape[1]
    words = words.reshape(g, 2, 128, t, 2).transpose(0, 2, 3, 1, 4)
    return np.concatenate([words.reshape(g, -1), scales.reshape(g, -1)], axis=1)


def unpack_table4(tab):
    g, t = tab.shape[0], tab.shape[1] // 544
    words = tab[:, :512 * t].reshape(g, 128, t, 2, 2).transpose(0, 3, 1, 2, 4).reshape(2 * g, 128, 2 * t)
    return unpack_weight(words, tab[:, 512 * t:].reshape(2 * g, 16, t), "e2m1")


K, R, N, T, S = 2048, 512, 256, 4096, 1024

def setup_inputs():
    n = np.random.standard_normal
    s = mx_kscale(K)[:, None]
    u = mx_kscale(R)[:, None]
    w0_words, w0_scales = pack_weight(n((K, N)) / np.sqrt(K) / s, "e2m1")
    return {
        "tab": pack_table4(n((K, T)) * s),
        "offs": striped(np.random.permutation(T)[:S]),
        "w0_words": w0_words,
        "w0_scales": w0_scales,
        "a": (n((K, R)) / np.sqrt(K) / s * u.T).astype(np.float32),
        "b": (n((R, N)) / np.sqrt(R) / u).astype(np.float32),
        "lam": np.exp(0.3 * n(R)).astype(np.float32),
        "bias": (0.5 * n(N)).astype(np.float32),
    }

def reference(tab, offs, w0_words, w0_scales, a, b, lam, bias):
    v = unpack_table4(tab)[:, unstriped(offs)]
    w0 = unpack_weight(w0_words, w0_scales, "e2m1")
    aq = mxq(f64(a), 0, "e4m3")
    h = f64(lam)[:, None] * (aq.T @ v)
    hq = mxq(h, 0, "e4m3")
    bq = mxq(f64(b), 0, "e4m3")
    y = w0.T @ v + bq.T @ hq
    return 1.0 / (1.0 + np.exp(-(y + f64(bias)[:, None])))

@@ -1,0 +1,254 @@
+from contextlib import ExitStack
+
+import concourse.mybir as mybir
+
+K, R, N, T, S = 2048, 512, 256, 4096, 1024
+FLOPS = 2 * S * (K * R + K * N + R * N)
+
+F32 = mybir.dt.float32
+BF16 = mybir.dt.bfloat16
+I32 = mybir.dt.int32
+U32 = mybir.dt.uint32
+U16 = mybir.dt.uint16
+U8 = mybir.dt.uint8
+FP8X4 = mybir.dt.float8_e4m3fn_x4
+FP4X4 = mybir.dt.float4_e2m1fn_x4
+ACT = mybir.ActivationFunctionType
+MULT = mybir.AluOpType.mult
+
+P = 128
+PACK = 4
+PASSES = K // (P * PACK)
+HALF = 512
+HALVES = S // HALF
+SHIFT_ROWS = 104
+
+
+def tile_list_adapter_moderation_probs_kernel(tc, tab, offs, w0_words, w0_scales, a, b, lam, bias, out):
+    nc = tc.nc
+    with ExitStack() as ctx:
+        keep = ctx.enter_context(tc.tile_pool(name="keep", bufs=1))
+        psum = ctx.enter_context(tc.psum_pool(name="psum", bufs=1))
+
+        def sb(name, shape, dtype):
+            return keep.tile(shape, dtype, name=name, align_bytes=64)
+
+        offsets = sb("offsets", [P, S // 16], U16)
+        nc.sync.dma_start(offsets[:], offs)
+
+        scale_win = sb("scale_win", [P, T], U8)
+        nc.vector.memset(scale_win[:].bitcast(I32), 0)
+        w0_plane = sb("w0_plane", [P, PASSES, N], U8)
+        nc.vector.memset(w0_plane[:].rearrange("p a n -> p (a n)").bitcast(I32), 0)
+        v_plane = [sb(f"v_plane{g}", [P, S], U8) for g in range(PASSES)]
+        for g in range(1, PASSES):
+            nc.vector.memset(v_plane[g][:].bitcast(I32), 0)
+
+        lam_sb = sb("lam_sb", [P, PACK], F32)
+        bias_sb = sb("bias_sb", [P, N // P], F32)
+        nc.scalar.dma_start(lam_sb[:], lam.rearrange("(p t) -> p t", t=PACK))
+        with nc.allow_non_contiguous_dma(reason="one bias value a partition"):
+            nc.scalar.dma_start(bias_sb[:], bias.rearrange("(u p) -> p u", p=P))
+        for q in range(4):
+            nc.scalar.dma_start(
+                w0_plane[32 * q : 32 * q + 4, :, :].bitcast(I32),
+                w0_scales[:, 4 * q : 4 * q + 4, :].rearrange("a r n -> r a n").bitcast(I32),
+            )
+        warm = sb("warm", [P, N // P], F32)
+        nc.scalar.activation(warm[:], bias_sb[:], ACT.Sigmoid)
+
+        for m in range(2):
+            rows = tab[m, 512 * T :].rearrange("(h q r t) -> r q h t", h=2, q=4, r=4)
+            for r in range(4):
+                nc.gpsimd.dma_start(scale_win[4 * m + r : P : 16, :].bitcast(I32), rows[r].bitcast(I32))
+
+        pieces = [1, 1, 2, 2]
+        a_raw = []
+        words_win = []
+
+        def load_a(g):
+            width = R // pieces[g]
+            src = a[512 * g : 512 * (g + 1), :].rearrange("(p j) r -> p j r", j=PACK)
+            tiles = []
+            for c in range(pieces[g]):
+                raw = sb(f"a_raw{g}_{c}", [P, PACK, width], F32)
+                nc.sync.dma_start(raw[:], src[:, :, c * width : (c + 1) * width])
+                tiles.append(raw)
+            a_raw.append(tiles)
+
+        def load_words(m):
+            win = sb(f"words_win{m}", [P, T], I32)
+            nc.sync.dma_start(win[:], tab[m, : 512 * T].rearrange("(p c) -> p c", p=P).bitcast(I32))
+            words_win.append(win)
+
+        load_a(0)
+        load_words(0)
+        load_a(1)
+        load_words(1)
+        load_a(2)
+        load_a(3)
+        w0_sb = sb("w0_sb", [P, PASSES, 2 * N], U8)
+        nc.sync.dma_start(w0_sb[:].bitcast(I32), w0_words.rearrange("a p c -> p a c").bitcast(I32))
+        b_raw = sb("b_raw", [P, PACK, N], F32)
+        nc.sync.dma_start(b_raw[:], b.rearrange("(p j) n -> p j n", j=PACK))
+
+        a_bf = [sb(f"a_bf{g}", [P, PACK, P, PACK], BF16) for g in range(PASSES)]
+        a_codes = [sb(f"a_codes{g}", [P, R], U32) for g in range(PASSES)]
+        a_plane = [sb(f"a_plane{g}", [P, R], U8) for g in range(PASSES)]
+
+        def cast_a(g, c, lo, hi, on_vector):
+            per = P // pieces[g]
+            dst = a_bf[g][:, :, c * per + lo : c * per + hi, :].rearrange("p t m j -> p m t j")
+            src = a_raw[g][c][:, :, 4 * lo : 4 * hi].rearrange("p j (m t) -> p m t j", t=PACK)
+            if on_vector:
+                nc.vector.tensor_copy(dst, src)
+            else:
+                nc.scalar.copy(dst, src)
+
+        def quant_a(g, parts):
+            flat = a_bf[g][:].rearrange("p t m j -> p (t m j)")
+            w = R // parts
+            for i in range(parts):
+                nc.vector.quantize_mx(
+                    out=a_codes[g][:, i * w : (i + 1) * w].bitcast(FP8X4),
+                    scales=a_plane[g][:, i * w : (i + 1) * w],
+                    in_=flat[:, 4 * i * w : 4 * (i + 1) * w],
+                )
+
+        v_words = {}
+
+        def gather_words(m):
+            picked = []
+            for hf in range(HALVES):
+                g = sb(f"picked{m}_{hf}", [P, HALF], I32)
+                nc.vector.tensor_copy(
+                    g[:].bitcast(U32), words_win[m][:].bitcast(U32).indirect(offsets[:, 32 * hf : 32 * (hf + 1)])
+                )
+                picked.append(g)
+            for hf in range(HALVES):
+                parted = sb(f"parted{m}_{hf}", [P, 2, HALF], U16)
+                nc.vector.tensor_copy(parted[:], picked[hf][:].bitcast(U16).rearrange("p (n h) -> p h n", h=2))
+                for h in range(2):
+                    v_words[2 * m + h, hf] = parted[:, h, :]
+
+        h_acc = {}
+        for hf in range(HALVES):
+            for t in range(PACK):
+                h_acc[hf, t] = psum.tile([P, HALF], F32, name=f"h_acc{hf}_{t}", tag=f"bank{4 * hf + t}")
+
+        def down_pass(g):
+            for hf in range(HALVES):
+                for t in range(PACK):
+                    nc.tensor.matmul_mx(
+                        out=h_acc[hf, t][:],
+                        lhsT=a_codes[g][:, P * t : P * (t + 1)].bitcast(FP8X4),
+                        lhsT_scale=a_plane[g][:, P * t : P * (t + 1)],
+                        rhs=v_words[g, hf].bitcast(FP4X4),
+                        rhs_scale=v_plane[g][:, HALF * hf : HALF * (hf + 1)],
+                        start=(g == 0),
+                        stop=(g == PASSES - 1),
+                    )
+
+        cast_a(0, 0, 0, P, False)
+        nc.vector.tensor_copy(v_plane[0][:], scale_win[:].indirect(offsets[:]))
+        for g in range(1, PASSES):
+            first = 16 * (g % 2) + 4 * (g // 2)
+            nc.gpsimd.dma_start(
+                v_plane[g][0:SHIFT_ROWS, :].bitcast(I32), v_plane[0][first : first + SHIFT_ROWS, :].bitcast(I32)
+            )
+        quant_a(0, 1)
+        gather_words(0)
+        down_pass(0)
+        cast_a(1, 0, 0, P, False)
+        quant_a(1, 1)
+        down_pass(1)
+        gather_words(1)
+        cast_a(2, 0, 0, 64, False)
+        cast_a(2, 1, 0, 64, False)
+        quant_a(2, 4)
+        down_pass(2)
+        cast_a(3, 0, 0, 40, True)
+        cast_a(3, 0, 40, 64, False)
+        cast_a(3, 1, 0, 40, True)
+        cast_a(3, 1, 40, 64, False)
+        quant_a(3, 4)
+        down_pass(3)
+
+        h_codes, h_plane = [], []
+        h_rows, h_mix = [], []
+        for hf in range(HALVES):
+            h_rows.append(sb(f"h_rows{hf}", [P, PACK, HALF], BF16))
+            h_mix.append(sb(f"h_mix{hf}", [P, HALF, PACK], BF16))
+            h_codes.append(sb(f"h_codes{hf}", [P, HALF], U32))
+            h_plane.append(sb(f"h_plane{hf}", [P, HALF], U8))
+
+        def evac_h(hf, t, on_vector):
+            if on_vector:
+                nc.vector.tensor_scalar(h_rows[hf][:, t, :], h_acc[hf, t][:], lam_sb[:, t : t + 1], None, op0=MULT)
+            else:
+                nc.scalar.activation(h_rows[hf][:, t, :], h_acc[hf, t][:], ACT.Copy, scale=lam_sb[:, t : t + 1])
+
+        def quant_h(hf):
+            nc.vector.tensor_copy(
+                h_mix[hf][:].rearrange("p (c i) t -> p c t i", i=4), h_rows[hf][:].rearrange("p t (c i) -> p c t i", i=4)
+            )
+            nc.vector.quantize_mx(
+                out=h_codes[hf][:].bitcast(FP8X4), scales=h_plane[hf][:], in_=h_mix[hf][:].rearrange("p n t -> p (n t)")
+            )
+
+        b_bf = sb("b_bf", [P, N, PACK], BF16)
+        b_codes = sb("b_codes", [P, N], U32)
+        b_plane = sb("b_plane", [P, N], U8)
+
+        for t in range(PACK):
+            evac_h(0, t, t % 2 == 1)
+        for t in range(PACK):
+            evac_h(1, t, False)
+        quant_h(0)
+        nc.vector.tensor_copy(
+            b_bf[:].rearrange("p (c i) j -> p c j i", i=4), b_raw[:].rearrange("p j (c i) -> p c j i", i=4)
+        )
+        nc.vector.quantize_mx(
+            out=b_codes[:].bitcast(FP8X4), scales=b_plane[:], in_=b_bf[:].rearrange("p n j -> p (n j)")
+        )
+        quant_h(1)
+
+        for hf in range(HALVES):
+            y_acc = [psum.tile([P, HALF], F32, name=f"y_acc{hf}_{u}", tag=f"bank{2 * hf + u}") for u in range(N // P)]
+
+            def base(u):
+                for g in range(PASSES):
+                    nc.tensor.matmul_mx(
+                        out=y_acc[u][:],
+                        lhsT=w0_sb[:, g, 2 * P * u : 2 * P * (u + 1)].bitcast(FP4X4),
+                        lhsT_scale=w0_plane[:, g, P * u : P * (u + 1)],
+                        rhs=v_words[g, hf].bitcast(FP4X4),
+                        rhs_scale=v_plane[g][:, HALF * hf : HALF * (hf + 1)],
+                        start=(g == 0),
+                        stop=False,
+                    )
+
+            def up(u):
+                nc.tensor.matmul_mx(
+                    out=y_acc[u][:],
+                    lhsT=b_codes[:, P * u : P * (u + 1)].bitcast(FP8X4),
+                    lhsT_scale=b_plane[:, P * u : P * (u + 1)],
+                    rhs=h_codes[hf][:].bitcast(FP8X4),
+                    rhs_scale=h_plane[hf][:],
+                    start=False,
+                    stop=True,
+                )
+                prob = sb(f"prob{hf}_{u}", [P, HALF], F32)
+                nc.scalar.activation(prob[:], y_acc[u][:], ACT.Sigmoid, bias=bias_sb[:, u : u + 1])
+                nc.sync.dma_start(out[P * u : P * (u + 1), HALF * hf : HALF * (hf + 1)], prob[:])
+
+            if hf == 0:
+                base(0)
+                base(1)
+                up(0)
+                up(1)
+            else:
+                base(0)
+                up(0)
+                base(1)
+                up(1)

@@ -21,7 +21,6 @@ PACK = 4
 PASSES = K // (P * PACK)
 HALF = 512
 HALVES = S // HALF
-SHIFT_ROWS = 104
 
 
 def tile_list_adapter_moderation_probs_kernel(tc, tab, offs, w0_words, w0_scales, a, b, lam, bias, out):
@@ -36,45 +35,48 @@ def tile_list_adapter_moderation_probs_kernel(tc, tab, offs, w0_words, w0_scales
         offsets = sb("offsets", [P, S // 16], U16)
         nc.sync.dma_start(offsets[:], offs)
 
-        scale_win = sb("scale_win", [P, T], U8)
-        nc.vector.memset(scale_win[:].bitcast(I32), 0)
+        scale_win = [sb(f"scale_win{m}", [P, T], U8) for m in range(2)]
+        for m in range(2):
+            nc.sync.dma_start(
+                scale_win[m][96:P, :].bitcast(I32), tab[m, 512 * T :].rearrange("(q t) -> q t", t=T).bitcast(I32)
+            )
+        for m in range(2):
+            nc.vector.memset(scale_win[m][0:96, :].bitcast(I32), 0)
         w0_plane = sb("w0_plane", [P, PASSES, N], U8)
-        nc.vector.memset(w0_plane[:].rearrange("p a n -> p (a n)").bitcast(I32), 0)
-        v_plane = [sb(f"v_plane{g}", [P, S], U8) for g in range(PASSES)]
-        for g in range(1, PASSES):
-            nc.vector.memset(v_plane[g][:].bitcast(I32), 0)
+        v_plane = [sb(f"v_plane{h}", [P, 2, S], U8) for h in range(2)]
+        warm = sb("warm", [P, 2], F32)
+        nc.gpsimd.memset(warm[:, 0:1], 0.0)
+        nc.scalar.activation(warm[:, 1:2], warm[:, 0:1], ACT.Sigmoid)
+        nc.gpsimd.memset(w0_plane[:].rearrange("p a n -> p (a n)").bitcast(I32), 0)
+        for h in range(2):
+            nc.gpsimd.memset(v_plane[h][:].rearrange("p m s -> p (m s)").bitcast(I32), 0)
 
         lam_sb = sb("lam_sb", [P, PACK], F32)
         bias_sb = sb("bias_sb", [P, N // P], F32)
-        nc.scalar.dma_start(lam_sb[:], lam.rearrange("(p t) -> p t", t=PACK))
+        nc.gpsimd.dma_start(lam_sb[:], lam.rearrange("(p t) -> p t", t=PACK))
         with nc.allow_non_contiguous_dma(reason="one bias value a partition"):
-            nc.scalar.dma_start(bias_sb[:], bias.rearrange("(u p) -> p u", p=P))
+            nc.gpsimd.dma_start(bias_sb[:], bias.rearrange("(u p) -> p u", p=P))
         for q in range(4):
-            nc.scalar.dma_start(
+            nc.gpsimd.dma_start(
                 w0_plane[32 * q : 32 * q + 4, :, :].bitcast(I32),
                 w0_scales[:, 4 * q : 4 * q + 4, :].rearrange("a r n -> r a n").bitcast(I32),
             )
-        warm = sb("warm", [P, N // P], F32)
-        nc.scalar.activation(warm[:], bias_sb[:], ACT.Sigmoid)
-
-        for m in range(2):
-            rows = tab[m, 512 * T :].rearrange("(h q r t) -> r q h t", h=2, q=4, r=4)
-            for r in range(4):
-                nc.gpsimd.dma_start(scale_win[4 * m + r : P : 16, :].bitcast(I32), rows[r].bitcast(I32))
 
         pieces = [1, 1, 2, 2]
-        a_raw = []
+        a_raw = {}
         words_win = []
+        stage = ctx.enter_context(tc.tile_pool(name="stage", bufs=1))
+        SLOT = 8192
 
         def load_a(g):
             width = R // pieces[g]
             src = a[512 * g : 512 * (g + 1), :].rearrange("(p j) r -> p j r", j=PACK)
             tiles = []
             for c in range(pieces[g]):
-                raw = sb(f"a_raw{g}_{c}", [P, PACK, width], F32)
+                raw = stage.tile([P, PACK, width], F32, name=f"a_raw{g}_{c}", align_bytes=64, offset=(g % 2) * SLOT + c * 16 * width)
                 nc.sync.dma_start(raw[:], src[:, :, c * width : (c + 1) * width])
                 tiles.append(raw)
-            a_raw.append(tiles)
+            a_raw[g] = tiles
 
         def load_words(m):
             win = sb(f"words_win{m}", [P, T], I32)
@@ -85,12 +87,6 @@ def tile_list_adapter_moderation_probs_kernel(tc, tab, offs, w0_words, w0_scales
         load_words(0)
         load_a(1)
         load_words(1)
-        load_a(2)
-        load_a(3)
-        w0_sb = sb("w0_sb", [P, PASSES, 2 * N], U8)
-        nc.sync.dma_start(w0_sb[:].bitcast(I32), w0_words.rearrange("a p c -> p a c").bitcast(I32))
-        b_raw = sb("b_raw", [P, PACK, N], F32)
-        nc.sync.dma_start(b_raw[:], b.rearrange("(p j) n -> p j n", j=PACK))
 
         a_bf = [sb(f"a_bf{g}", [P, PACK, P, PACK], BF16) for g in range(PASSES)]
         a_codes = [sb(f"a_codes{g}", [P, R], U32) for g in range(PASSES)]
@@ -144,27 +140,38 @@ def tile_list_adapter_moderation_probs_kernel(tc, tab, offs, w0_words, w0_scales
                         lhsT=a_codes[g][:, P * t : P * (t + 1)].bitcast(FP8X4),
                         lhsT_scale=a_plane[g][:, P * t : P * (t + 1)],
                         rhs=v_words[g, hf].bitcast(FP4X4),
-                        rhs_scale=v_plane[g][:, HALF * hf : HALF * (hf + 1)],
+                        rhs_scale=v_plane[g % 2][:, g // 2, HALF * hf : HALF * (hf + 1)],
                         start=(g == 0),
                         stop=(g == PASSES - 1),
                     )
 
+        picked_scales = sb("picked_scales", [P, 2, S], U8)
+        for m in range(2):
+            nc.vector.tensor_copy(picked_scales[:, m, :], scale_win[m][:].indirect(offsets[:]))
         cast_a(0, 0, 0, P, False)
-        nc.vector.tensor_copy(v_plane[0][:], scale_win[:].indirect(offsets[:]))
-        for g in range(1, PASSES):
-            first = 16 * (g % 2) + 4 * (g // 2)
-            nc.gpsimd.dma_start(
-                v_plane[g][0:SHIFT_ROWS, :].bitcast(I32), v_plane[0][first : first + SHIFT_ROWS, :].bitcast(I32)
-            )
+        for h in range(2):
+            queue = nc.scalar if h == 0 else nc.gpsimd
+            for q in range(4):
+                first = 96 + 16 * h + 4 * q
+                queue.dma_start(
+                    v_plane[h][32 * q : 32 * q + 4, :, :].rearrange("p m s -> p (m s)").bitcast(I32),
+                    picked_scales[first : first + 4, :, :].rearrange("p m s -> p (m s)").bitcast(I32),
+                )
+        load_a(2)
         quant_a(0, 1)
         gather_words(0)
         down_pass(0)
         cast_a(1, 0, 0, P, False)
+        load_a(3)
         quant_a(1, 1)
         down_pass(1)
         gather_words(1)
         cast_a(2, 0, 0, 64, False)
+        w0_sb = stage.tile([P, PASSES, 2 * N], U8, name="w0_sb", align_bytes=64, offset=0)
+        nc.sync.dma_start(w0_sb[:].bitcast(I32), w0_words.rearrange("a p c -> p a c").bitcast(I32))
         cast_a(2, 1, 0, 64, False)
+        b_raw = stage.tile([P, PACK, N], F32, name="b_raw", align_bytes=64, offset=SLOT // 2)
+        nc.sync.dma_start(b_raw[:], b.rearrange("(p j) n -> p j n", j=PACK))
         quant_a(2, 4)
         down_pass(2)
         cast_a(3, 0, 0, 40, True)
@@ -223,7 +230,7 @@ def tile_list_adapter_moderation_probs_kernel(tc, tab, offs, w0_words, w0_scales
                         lhsT=w0_sb[:, g, 2 * P * u : 2 * P * (u + 1)].bitcast(FP4X4),
                         lhsT_scale=w0_plane[:, g, P * u : P * (u + 1)],
                         rhs=v_words[g, hf].bitcast(FP4X4),
-                        rhs_scale=v_plane[g][:, HALF * hf : HALF * (hf + 1)],
+                        rhs_scale=v_plane[g % 2][:, g // 2, HALF * hf : HALF * (hf + 1)],
                         start=(g == 0),
                         stop=False,
                     )

@@ -62,24 +62,24 @@ def tile_list_adapter_moderation_probs_kernel(tc, tab, offs, w0_words, w0_scales
                 w0_scales[:, 4 * q : 4 * q + 4, :].rearrange("a r n -> r a n").bitcast(I32),
             )
 
-        pieces = [1, 1, 2, 2]
         a_raw = {}
         words_win = []
         stage = ctx.enter_context(tc.tile_pool(name="stage", bufs=1))
-        SLOT = 8192
+        KB = 1024
+        A_AT = [0, 8 * KB, 16 * KB, 8 * KB]
+        PICKED_AT = [16 * KB, 24 * KB]
+        WORDS_AT = [28 * KB, 44 * KB]
+
+        def staged(name, shape, dtype, at):
+            return stage.tile(shape, dtype, name=name, align_bytes=64, offset=at)
 
         def load_a(g):
-            width = R // pieces[g]
-            src = a[512 * g : 512 * (g + 1), :].rearrange("(p j) r -> p j r", j=PACK)
-            tiles = []
-            for c in range(pieces[g]):
-                raw = stage.tile([P, PACK, width], F32, name=f"a_raw{g}_{c}", align_bytes=64, offset=(g % 2) * SLOT + c * 16 * width)
-                nc.sync.dma_start(raw[:], src[:, :, c * width : (c + 1) * width])
-                tiles.append(raw)
-            a_raw[g] = tiles
+            raw = staged(f"a_raw{g}", [P, PACK, R], F32, A_AT[g])
+            nc.sync.dma_start(raw[:], a[512 * g : 512 * (g + 1), :].rearrange("(p j) r -> p j r", j=PACK))
+            a_raw[g] = raw
 
         def load_words(m):
-            win = sb(f"words_win{m}", [P, T], I32)
+            win = staged(f"words_win{m}", [P, T], I32, WORDS_AT[m])
             nc.sync.dma_start(win[:], tab[m, : 512 * T].rearrange("(p c) -> p c", p=P).bitcast(I32))
             words_win.append(win)
 
@@ -92,10 +92,9 @@ def tile_list_adapter_moderation_probs_kernel(tc, tab, offs, w0_words, w0_scales
         a_codes = [sb(f"a_codes{g}", [P, R], U32) for g in range(PASSES)]
         a_plane = [sb(f"a_plane{g}", [P, R], U8) for g in range(PASSES)]
 
-        def cast_a(g, c, lo, hi, on_vector):
-            per = P // pieces[g]
-            dst = a_bf[g][:, :, c * per + lo : c * per + hi, :].rearrange("p t m j -> p m t j")
-            src = a_raw[g][c][:, :, 4 * lo : 4 * hi].rearrange("p j (m t) -> p m t j", t=PACK)
+        def cast_a(g, lo, hi, on_vector):
+            dst = a_bf[g][:, :, lo:hi, :].rearrange("p t m j -> p m j t")
+            src = a_raw[g][:, :, 4 * lo : 4 * hi].rearrange("p j (m t) -> p m j t", t=PACK)
             if on_vector:
                 nc.vector.tensor_copy(dst, src)
             else:
@@ -116,7 +115,7 @@ def tile_list_adapter_moderation_probs_kernel(tc, tab, offs, w0_words, w0_scales
         def gather_words(m):
             picked = []
             for hf in range(HALVES):
-                g = sb(f"picked{m}_{hf}", [P, HALF], I32)
+                g = staged(f"picked{m}_{hf}", [P, HALF], I32, PICKED_AT[m] + 2 * KB * hf)
                 nc.vector.tensor_copy(
                     g[:].bitcast(U32), words_win[m][:].bitcast(U32).indirect(offsets[:, 32 * hf : 32 * (hf + 1)])
                 )
@@ -148,36 +147,34 @@ def tile_list_adapter_moderation_probs_kernel(tc, tab, offs, w0_words, w0_scales
         picked_scales = sb("picked_scales", [P, 2, S], U8)
         for m in range(2):
             nc.vector.tensor_copy(picked_scales[:, m, :], scale_win[m][:].indirect(offsets[:]))
-        cast_a(0, 0, 0, P, False)
+        cast_a(0, 0, P, False)
         for h in range(2):
-            queue = nc.scalar if h == 0 else nc.gpsimd
             for q in range(4):
+                queue = nc.scalar if 4 * h + q < 6 else nc.gpsimd
                 first = 96 + 16 * h + 4 * q
                 queue.dma_start(
                     v_plane[h][32 * q : 32 * q + 4, :, :].rearrange("p m s -> p (m s)").bitcast(I32),
                     picked_scales[first : first + 4, :, :].rearrange("p m s -> p (m s)").bitcast(I32),
                 )
-        load_a(2)
         quant_a(0, 1)
         gather_words(0)
+        load_a(2)
         down_pass(0)
-        cast_a(1, 0, 0, P, False)
+        cast_a(1, 0, P, False)
         load_a(3)
         quant_a(1, 1)
         down_pass(1)
         gather_words(1)
-        cast_a(2, 0, 0, 64, False)
-        w0_sb = stage.tile([P, PASSES, 2 * N], U8, name="w0_sb", align_bytes=64, offset=0)
+        w0_sb = staged("w0_sb", [P, PASSES, 2 * N], U8, WORDS_AT[1])
         nc.sync.dma_start(w0_sb[:].bitcast(I32), w0_words.rearrange("a p c -> p a c").bitcast(I32))
-        cast_a(2, 1, 0, 64, False)
-        b_raw = stage.tile([P, PACK, N], F32, name="b_raw", align_bytes=64, offset=SLOT // 2)
+        b_raw = staged("b_raw", [P, PACK, N], F32, WORDS_AT[1] + 2 * KB)
         nc.sync.dma_start(b_raw[:], b.rearrange("(p j) n -> p j n", j=PACK))
+        cast_a(2, 0, 80, False)
+        cast_a(2, 80, P, True)
         quant_a(2, 4)
         down_pass(2)
-        cast_a(3, 0, 0, 40, True)
-        cast_a(3, 0, 40, 64, False)
-        cast_a(3, 1, 0, 40, True)
-        cast_a(3, 1, 40, 64, False)
+        cast_a(3, 0, 48, False)
+        cast_a(3, 48, P, True)
         quant_a(3, 4)
         down_pass(3)
 
@@ -220,42 +217,40 @@ def tile_list_adapter_moderation_probs_kernel(tc, tab, offs, w0_words, w0_scales
         )
         quant_h(1)
 
-        for hf in range(HALVES):
-            y_acc = [psum.tile([P, HALF], F32, name=f"y_acc{hf}_{u}", tag=f"bank{2 * hf + u}") for u in range(N // P)]
-
-            def base(u):
-                for g in range(PASSES):
-                    nc.tensor.matmul_mx(
-                        out=y_acc[u][:],
-                        lhsT=w0_sb[:, g, 2 * P * u : 2 * P * (u + 1)].bitcast(FP4X4),
-                        lhsT_scale=w0_plane[:, g, P * u : P * (u + 1)],
-                        rhs=v_words[g, hf].bitcast(FP4X4),
-                        rhs_scale=v_plane[g % 2][:, g // 2, HALF * hf : HALF * (hf + 1)],
-                        start=(g == 0),
-                        stop=False,
-                    )
-
-            def up(u):
+        def base(acc, u, lo, hi):
+            hf, c = divmod(lo, HALF)
+            for g in range(PASSES):
                 nc.tensor.matmul_mx(
-                    out=y_acc[u][:],
-                    lhsT=b_codes[:, P * u : P * (u + 1)].bitcast(FP8X4),
-                    lhsT_scale=b_plane[:, P * u : P * (u + 1)],
-                    rhs=h_codes[hf][:].bitcast(FP8X4),
-                    rhs_scale=h_plane[hf][:],
-                    start=False,
-                    stop=True,
+                    out=acc[:, : hi - lo],
+                    lhsT=w0_sb[:, g, 2 * P * u : 2 * P * (u + 1)].bitcast(FP4X4),
+                    lhsT_scale=w0_plane[:, g, P * u : P * (u + 1)],
+                    rhs=v_words[g, hf][:, c : c + hi - lo].bitcast(FP4X4),
+                    rhs_scale=v_plane[g % 2][:, g // 2, lo:hi],
+                    start=(g == 0),
+                    stop=False,
                 )
-                prob = sb(f"prob{hf}_{u}", [P, HALF], F32)
-                nc.scalar.activation(prob[:], y_acc[u][:], ACT.Sigmoid, bias=bias_sb[:, u : u + 1])
-                nc.sync.dma_start(out[P * u : P * (u + 1), HALF * hf : HALF * (hf + 1)], prob[:])
 
-            if hf == 0:
-                base(0)
-                base(1)
-                up(0)
-                up(1)
-            else:
-                base(0)
-                up(0)
-                base(1)
-                up(1)
+        def up(acc, u, lo, hi):
+            hf, c = divmod(lo, HALF)
+            nc.tensor.matmul_mx(
+                out=acc[:, : hi - lo],
+                lhsT=b_codes[:, P * u : P * (u + 1)].bitcast(FP8X4),
+                lhsT_scale=b_plane[:, P * u : P * (u + 1)],
+                rhs=h_codes[hf][:, c : c + hi - lo].bitcast(FP8X4),
+                rhs_scale=h_plane[hf][:, c : c + hi - lo],
+                start=False,
+                stop=True,
+            )
+            prob = sb(f"prob{u}_{lo}", [P, hi - lo], F32)
+            nc.scalar.activation(prob[:], acc[:, : hi - lo], ACT.Sigmoid, bias=bias_sb[:, u : u + 1])
+            nc.sync.dma_start(out[P * u : P * (u + 1), lo:hi], prob[:])
+
+        blocks = [(0, 0, 512), (1, 0, 512), (0, 512, 1024), (1, 512, 768), (1, 768, 1024)]
+        y_acc = [psum.tile([P, HALF], F32, name=f"y_acc{i}", tag=f"bank{i}") for i in range(len(blocks))]
+        base(y_acc[0], *blocks[0])
+        base(y_acc[1], *blocks[1])
+        up(y_acc[0], *blocks[0])
+        up(y_acc[1], *blocks[1])
+        for i in range(2, len(blocks)):
+            base(y_acc[i], *blocks[i])
+            up(y_acc[i], *blocks[i])

@@ -35,27 +35,35 @@ def tile_list_adapter_moderation_probs_kernel(tc, tab, offs, w0_words, w0_scales
         offsets = sb("offsets", [P, S // 16], U16)
         nc.sync.dma_start(offsets[:], offs)
 
-        scale_win = [sb(f"scale_win{m}", [P, T], U8) for m in range(2)]
+        stage = ctx.enter_context(tc.tile_pool(name="stage", bufs=1))
+        KB = 1024
+        A_AT = [0, 8 * KB, 42 * KB, 50 * KB]
+        SCALE_AT = [58 * KB, 14 * KB]
+        PICKED_AT = [34 * KB, 38 * KB]
+        B_AT = 33 * KB
+        LAM_AT = 37 * KB
+        BIAS_AT = 37 * KB + 64
+        WORDS_AT = [42 * KB, 16 * KB]
+
+        def staged(name, shape, dtype, at):
+            return stage.tile(shape, dtype, name=name, align_bytes=64, offset=at)
+
+        scale_win = [staged(f"scale_win{m}", [P, T], U8, SCALE_AT[m]) for m in range(2)]
         for m in range(2):
             nc.sync.dma_start(
                 scale_win[m][96:P, :].bitcast(I32), tab[m, 512 * T :].rearrange("(q t) -> q t", t=T).bitcast(I32)
             )
+        warm = sb("warm", [P, 2], F32)
+        nc.vector.memset(warm[:, 0:1], 0.0)
+        nc.scalar.activation(warm[:, 1:2], warm[:, 0:1], ACT.Sigmoid)
         for m in range(2):
             nc.vector.memset(scale_win[m][0:96, :].bitcast(I32), 0)
-        w0_plane = sb("w0_plane", [P, PASSES, N], U8)
         v_plane = [sb(f"v_plane{h}", [P, 2, S], U8) for h in range(2)]
-        warm = sb("warm", [P, 2], F32)
-        nc.gpsimd.memset(warm[:, 0:1], 0.0)
-        nc.scalar.activation(warm[:, 1:2], warm[:, 0:1], ACT.Sigmoid)
-        nc.gpsimd.memset(w0_plane[:].rearrange("p a n -> p (a n)").bitcast(I32), 0)
         for h in range(2):
             nc.gpsimd.memset(v_plane[h][:].rearrange("p m s -> p (m s)").bitcast(I32), 0)
 
-        lam_sb = sb("lam_sb", [P, PACK], F32)
-        bias_sb = sb("bias_sb", [P, N // P], F32)
-        nc.gpsimd.dma_start(lam_sb[:], lam.rearrange("(p t) -> p t", t=PACK))
-        with nc.allow_non_contiguous_dma(reason="one bias value a partition"):
-            nc.gpsimd.dma_start(bias_sb[:], bias.rearrange("(u p) -> p u", p=P))
+        w0_plane = sb("w0_plane", [P, PASSES, N], U8)
+        nc.gpsimd.memset(w0_plane[:].rearrange("p a n -> p (a n)").bitcast(I32), 0)
         for q in range(4):
             nc.gpsimd.dma_start(
                 w0_plane[32 * q : 32 * q + 4, :, :].bitcast(I32),
@@ -64,14 +72,6 @@ def tile_list_adapter_moderation_probs_kernel(tc, tab, offs, w0_words, w0_scales
 
         a_raw = {}
         words_win = []
-        stage = ctx.enter_context(tc.tile_pool(name="stage", bufs=1))
-        KB = 1024
-        A_AT = [0, 8 * KB, 16 * KB, 8 * KB]
-        PICKED_AT = [16 * KB, 24 * KB]
-        WORDS_AT = [28 * KB, 44 * KB]
-
-        def staged(name, shape, dtype, at):
-            return stage.tile(shape, dtype, name=name, align_bytes=64, offset=at)
 
         def load_a(g):
             raw = staged(f"a_raw{g}", [P, PACK, R], F32, A_AT[g])
@@ -85,8 +85,8 @@ def tile_list_adapter_moderation_probs_kernel(tc, tab, offs, w0_words, w0_scales
 
         load_a(0)
         load_words(0)
-        load_a(1)
-        load_words(1)
+        w0_sb = sb("w0_sb", [P, PASSES, 2 * N], U8)
+        nc.sync.dma_start(w0_sb[:].bitcast(I32), w0_words.rearrange("a p c -> p a c").bitcast(I32))
 
         a_bf = [sb(f"a_bf{g}", [P, PACK, P, PACK], BF16) for g in range(PASSES)]
         a_codes = [sb(f"a_codes{g}", [P, R], U32) for g in range(PASSES)]
@@ -127,56 +127,54 @@ def tile_list_adapter_moderation_probs_kernel(tc, tab, offs, w0_words, w0_scales
                     v_words[2 * m + h, hf] = parted[:, h, :]
 
         h_acc = {}
-        for hf in range(HALVES):
-            for t in range(PACK):
-                h_acc[hf, t] = psum.tile([P, HALF], F32, name=f"h_acc{hf}_{t}", tag=f"bank{4 * hf + t}")
+
+        def bank(name, i):
+            return psum.tile([P, HALF], F32, name=name, tag=f"bank{i}")
+
+        early = [(0, 0), (0, 1), (0, 2), (0, 3), (1, 0), (1, 1)]
+        for i, (hf, t) in enumerate(early):
+            h_acc[hf, t] = bank(f"h_acc{hf}_{t}", i)
+
+        def down(g, hf, t):
+            nc.tensor.matmul_mx(
+                out=h_acc[hf, t][:],
+                lhsT=a_codes[g][:, P * t : P * (t + 1)].bitcast(FP8X4),
+                lhsT_scale=a_plane[g][:, P * t : P * (t + 1)],
+                rhs=v_words[g, hf].bitcast(FP4X4),
+                rhs_scale=v_plane[g % 2][:, g // 2, HALF * hf : HALF * (hf + 1)],
+                start=(g == 0),
+                stop=(g == PASSES - 1),
+            )
 
         def down_pass(g):
-            for hf in range(HALVES):
-                for t in range(PACK):
-                    nc.tensor.matmul_mx(
-                        out=h_acc[hf, t][:],
-                        lhsT=a_codes[g][:, P * t : P * (t + 1)].bitcast(FP8X4),
-                        lhsT_scale=a_plane[g][:, P * t : P * (t + 1)],
-                        rhs=v_words[g, hf].bitcast(FP4X4),
-                        rhs_scale=v_plane[g % 2][:, g // 2, HALF * hf : HALF * (hf + 1)],
-                        start=(g == 0),
-                        stop=(g == PASSES - 1),
-                    )
+            for hf, t in early:
+                down(g, hf, t)
 
         picked_scales = sb("picked_scales", [P, 2, S], U8)
         for m in range(2):
             nc.vector.tensor_copy(picked_scales[:, m, :], scale_win[m][:].indirect(offsets[:]))
         cast_a(0, 0, P, False)
-        for h in range(2):
-            for q in range(4):
-                queue = nc.scalar if 4 * h + q < 6 else nc.gpsimd
-                first = 96 + 16 * h + 4 * q
-                queue.dma_start(
-                    v_plane[h][32 * q : 32 * q + 4, :, :].rearrange("p m s -> p (m s)").bitcast(I32),
-                    picked_scales[first : first + 4, :, :].rearrange("p m s -> p (m s)").bitcast(I32),
-                )
+        for move in range(8):
+            h, q = divmod(move, 4)
+            if move == 4:
+                load_words(1)
+            first = 96 + 16 * h + 4 * q
+            nc.sync.dma_start(
+                v_plane[h][32 * q : 32 * q + 4, :, :].rearrange("p m s -> p (m s)").bitcast(I32),
+                picked_scales[first : first + 4, :, :].rearrange("p m s -> p (m s)").bitcast(I32),
+            )
+        load_a(1)
         quant_a(0, 1)
         gather_words(0)
         load_a(2)
-        down_pass(0)
-        cast_a(1, 0, P, False)
         load_a(3)
-        quant_a(1, 1)
-        down_pass(1)
-        gather_words(1)
-        w0_sb = staged("w0_sb", [P, PASSES, 2 * N], U8, WORDS_AT[1])
-        nc.sync.dma_start(w0_sb[:].bitcast(I32), w0_words.rearrange("a p c -> p a c").bitcast(I32))
-        b_raw = staged("b_raw", [P, PACK, N], F32, WORDS_AT[1] + 2 * KB)
+        lam_sb = staged("lam_sb", [P, PACK], F32, LAM_AT)
+        nc.sync.dma_start(lam_sb[:], lam.rearrange("(p t) -> p t", t=PACK))
+        b_raw = staged("b_raw", [P, PACK, N], F32, B_AT)
         nc.sync.dma_start(b_raw[:], b.rearrange("(p j) n -> p j n", j=PACK))
-        cast_a(2, 0, 80, False)
-        cast_a(2, 80, P, True)
-        quant_a(2, 4)
-        down_pass(2)
-        cast_a(3, 0, 48, False)
-        cast_a(3, 48, P, True)
-        quant_a(3, 4)
-        down_pass(3)
+        bias_sb = staged("bias_sb", [P, N // P], F32, BIAS_AT)
+        with nc.allow_non_contiguous_dma(reason="one bias value a partition"):
+            nc.sync.dma_start(bias_sb[:], bias.rearrange("(u p) -> p u", p=P))
 
         h_codes, h_plane = [], []
         h_rows, h_mix = [], []
@@ -192,30 +190,20 @@ def tile_list_adapter_moderation_probs_kernel(tc, tab, offs, w0_words, w0_scales
             else:
                 nc.scalar.activation(h_rows[hf][:, t, :], h_acc[hf, t][:], ACT.Copy, scale=lam_sb[:, t : t + 1])
 
-        def quant_h(hf):
+        def quant_h(hf, lo, hi):
             nc.vector.tensor_copy(
-                h_mix[hf][:].rearrange("p (c i) t -> p c t i", i=4), h_rows[hf][:].rearrange("p t (c i) -> p c t i", i=4)
+                h_mix[hf][:, lo:hi, :].rearrange("p (c i) t -> p c t i", i=4),
+                h_rows[hf][:, :, lo:hi].rearrange("p t (c i) -> p c t i", i=4),
             )
             nc.vector.quantize_mx(
-                out=h_codes[hf][:].bitcast(FP8X4), scales=h_plane[hf][:], in_=h_mix[hf][:].rearrange("p n t -> p (n t)")
+                out=h_codes[hf][:, lo:hi].bitcast(FP8X4),
+                scales=h_plane[hf][:, lo:hi],
+                in_=h_mix[hf][:, lo:hi, :].rearrange("p n t -> p (n t)"),
             )
 
         b_bf = sb("b_bf", [P, N, PACK], BF16)
         b_codes = sb("b_codes", [P, N], U32)
         b_plane = sb("b_plane", [P, N], U8)
-
-        for t in range(PACK):
-            evac_h(0, t, t % 2 == 1)
-        for t in range(PACK):
-            evac_h(1, t, False)
-        quant_h(0)
-        nc.vector.tensor_copy(
-            b_bf[:].rearrange("p (c i) j -> p c j i", i=4), b_raw[:].rearrange("p j (c i) -> p c j i", i=4)
-        )
-        nc.vector.quantize_mx(
-            out=b_codes[:].bitcast(FP8X4), scales=b_plane[:], in_=b_bf[:].rearrange("p n j -> p (n j)")
-        )
-        quant_h(1)
 
         def base(acc, u, lo, hi):
             hf, c = divmod(lo, HALF)
@@ -245,12 +233,40 @@ def tile_list_adapter_moderation_probs_kernel(tc, tab, offs, w0_words, w0_scales
             nc.scalar.activation(prob[:], acc[:, : hi - lo], ACT.Sigmoid, bias=bias_sb[:, u : u + 1])
             nc.sync.dma_start(out[P * u : P * (u + 1), lo:hi], prob[:])
 
-        blocks = [(0, 0, 512), (1, 0, 512), (0, 512, 1024), (1, 512, 768), (1, 768, 1024)]
-        y_acc = [psum.tile([P, HALF], F32, name=f"y_acc{i}", tag=f"bank{i}") for i in range(len(blocks))]
-        base(y_acc[0], *blocks[0])
-        base(y_acc[1], *blocks[1])
-        up(y_acc[0], *blocks[0])
-        up(y_acc[1], *blocks[1])
-        for i in range(2, len(blocks)):
-            base(y_acc[i], *blocks[i])
-            up(y_acc[i], *blocks[i])
+        down_pass(0)
+        gather_words(1)
+        y_first = [bank(f"y_first{u}", 6 + u) for u in range(2)]
+        for u in range(2):
+            base(y_first[u], u, 0, HALF)
+        for g, split, parts in ((1, 80, 1), (2, 64, 1), (3, 44, 2)):
+            cast_a(g, 0, split, False)
+            cast_a(g, split, P, True)
+            quant_a(g, parts)
+            down_pass(g)
+
+        nc.vector.tensor_copy(
+            b_bf[:].rearrange("p (c i) j -> p c j i", i=4), b_raw[:].rearrange("p j (c i) -> p c j i", i=4)
+        )
+        nc.vector.quantize_mx(
+            out=b_codes[:].bitcast(FP8X4), scales=b_plane[:], in_=b_bf[:].rearrange("p n j -> p (n j)")
+        )
+        for t in range(PACK):
+            evac_h(0, t, t == 3)
+        quant_h(0, 0, HALF)
+        for t in range(2):
+            evac_h(1, t, False)
+        for t in range(2, PACK):
+            h_acc[1, t] = bank(f"h_acc1_{t}", t - 2)
+            for g in range(PASSES):
+                down(g, 1, t)
+            evac_h(1, t, False)
+        for u in range(2):
+            up(y_first[u], u, 0, HALF)
+        for c in range(2):
+            lo = HALF + 256 * c
+            quant_h(1, 256 * c, 256 * (c + 1))
+            y_rest = [bank(f"y_rest{c}_{u}", 2 + 2 * c + u) for u in range(2)]
+            for u in range(2):
+                base(y_rest[u], u, lo, lo + 256)
+            for u in range(2):
+                up(y_rest[u], u, lo, lo + 256)

@@ -37,56 +37,54 @@ def tile_list_adapter_moderation_probs_kernel(tc, tab, offs, w0_words, w0_scales
 
         stage = ctx.enter_context(tc.tile_pool(name="stage", bufs=1))
         KB = 1024
-        A_AT = [0, 8 * KB, 42 * KB, 50 * KB]
-        SCALE_AT = [58 * KB, 14 * KB]
-        PICKED_AT = [34 * KB, 38 * KB]
-        B_AT = 33 * KB
-        LAM_AT = 37 * KB
-        BIAS_AT = 37 * KB + 64
-        WORDS_AT = [42 * KB, 16 * KB]
+        A_AT = [0, 10 * KB, 24 * KB, 32 * KB]
+        PICKED_AT = [7 * KB, 19 * KB]
+        B_AT = 18 * KB
+        LAM_AT = 22 * KB
+        BIAS_AT = 22 * KB + 64
+        WORDS_AT = [24 * KB, 40 * KB]
 
         def staged(name, shape, dtype, at):
             return stage.tile(shape, dtype, name=name, align_bytes=64, offset=at)
 
-        scale_win = [staged(f"scale_win{m}", [P, T], U8, SCALE_AT[m]) for m in range(2)]
+        words_win = [staged(f"words_win{m}", [P, T], I32, WORDS_AT[m]) for m in range(2)]
+        scale_win = [words_win[1][:, T // 2 + m * T // 4 : T // 2 + (m + 1) * T // 4] for m in range(2)]
         for m in range(2):
             nc.sync.dma_start(
-                scale_win[m][96:P, :].bitcast(I32), tab[m, 512 * T :].rearrange("(q t) -> q t", t=T).bitcast(I32)
+                scale_win[m][96:P, :], tab[m, 512 * T :].rearrange("(q t) -> q t", t=T).bitcast(I32)
             )
+        w0_plane = sb("w0_plane", [P, PASSES, N], U8)
+        nc.gpsimd.memset(w0_plane[:].rearrange("p a n -> p (a n)").bitcast(I32), 0)
         warm = sb("warm", [P, 2], F32)
         nc.vector.memset(warm[:, 0:1], 0.0)
-        nc.scalar.activation(warm[:, 1:2], warm[:, 0:1], ACT.Sigmoid)
         for m in range(2):
-            nc.vector.memset(scale_win[m][0:96, :].bitcast(I32), 0)
+            nc.vector.memset(scale_win[m][0:96, :], 0)
         v_plane = [sb(f"v_plane{h}", [P, 2, S], U8) for h in range(2)]
         for h in range(2):
             nc.gpsimd.memset(v_plane[h][:].rearrange("p m s -> p (m s)").bitcast(I32), 0)
 
-        w0_plane = sb("w0_plane", [P, PASSES, N], U8)
-        nc.gpsimd.memset(w0_plane[:].rearrange("p a n -> p (a n)").bitcast(I32), 0)
         for q in range(4):
             nc.gpsimd.dma_start(
                 w0_plane[32 * q : 32 * q + 4, :, :].bitcast(I32),
                 w0_scales[:, 4 * q : 4 * q + 4, :].rearrange("a r n -> r a n").bitcast(I32),
             )
+        nc.scalar.activation(warm[:, 1:2], warm[:, 0:1], ACT.Sigmoid)
 
         a_raw = {}
-        words_win = []
 
         def load_a(g):
             raw = staged(f"a_raw{g}", [P, PACK, R], F32, A_AT[g])
             nc.sync.dma_start(raw[:], a[512 * g : 512 * (g + 1), :].rearrange("(p j) r -> p j r", j=PACK))
             a_raw[g] = raw
 
-        def load_words(m):
-            win = staged(f"words_win{m}", [P, T], I32, WORDS_AT[m])
-            nc.sync.dma_start(win[:], tab[m, : 512 * T].rearrange("(p c) -> p c", p=P).bitcast(I32))
-            words_win.append(win)
+        def load_words(m, lo, hi):
+            words = tab[m, : 512 * T].rearrange("(p c) -> p c", p=P).bitcast(I32)
+            nc.sync.dma_start(words_win[m][:, lo:hi], words[:, lo:hi])
 
-        load_a(0)
-        load_words(0)
+        load_words(0, 0, T)
         w0_sb = sb("w0_sb", [P, PASSES, 2 * N], U8)
         nc.sync.dma_start(w0_sb[:].bitcast(I32), w0_words.rearrange("a p c -> p a c").bitcast(I32))
+        load_words(1, 0, T // 2)
 
         a_bf = [sb(f"a_bf{g}", [P, PACK, P, PACK], BF16) for g in range(PASSES)]
         a_codes = [sb(f"a_codes{g}", [P, R], U32) for g in range(PASSES)]
@@ -113,16 +111,13 @@ def tile_list_adapter_moderation_probs_kernel(tc, tab, offs, w0_words, w0_scales
         v_words = {}
 
         def gather_words(m):
-            picked = []
             for hf in range(HALVES):
                 g = staged(f"picked{m}_{hf}", [P, HALF], I32, PICKED_AT[m] + 2 * KB * hf)
                 nc.vector.tensor_copy(
                     g[:].bitcast(U32), words_win[m][:].bitcast(U32).indirect(offsets[:, 32 * hf : 32 * (hf + 1)])
                 )
-                picked.append(g)
-            for hf in range(HALVES):
                 parted = sb(f"parted{m}_{hf}", [P, 2, HALF], U16)
-                nc.vector.tensor_copy(parted[:], picked[hf][:].bitcast(U16).rearrange("p (n h) -> p h n", h=2))
+                nc.vector.tensor_copy(parted[:], g[:].bitcast(U16).rearrange("p (n h) -> p h n", h=2))
                 for h in range(2):
                     v_words[2 * m + h, hf] = parted[:, h, :]
 
@@ -152,29 +147,21 @@ def tile_list_adapter_moderation_probs_kernel(tc, tab, offs, w0_words, w0_scales
 
         picked_scales = sb("picked_scales", [P, 2, S], U8)
         for m in range(2):
-            nc.vector.tensor_copy(picked_scales[:, m, :], scale_win[m][:].indirect(offsets[:]))
-        cast_a(0, 0, P, False)
+            nc.vector.tensor_copy(picked_scales[:, m, :], scale_win[m].bitcast(U8).indirect(offsets[:]))
         for move in range(8):
             h, q = divmod(move, 4)
-            if move == 4:
-                load_words(1)
+            if move == 3:
+                load_words(1, T // 2, T)
             first = 96 + 16 * h + 4 * q
             nc.sync.dma_start(
                 v_plane[h][32 * q : 32 * q + 4, :, :].rearrange("p m s -> p (m s)").bitcast(I32),
                 picked_scales[first : first + 4, :, :].rearrange("p m s -> p (m s)").bitcast(I32),
             )
-        load_a(1)
-        quant_a(0, 1)
         gather_words(0)
+        load_a(0)
+        load_a(1)
         load_a(2)
         load_a(3)
-        lam_sb = staged("lam_sb", [P, PACK], F32, LAM_AT)
-        nc.sync.dma_start(lam_sb[:], lam.rearrange("(p t) -> p t", t=PACK))
-        b_raw = staged("b_raw", [P, PACK, N], F32, B_AT)
-        nc.sync.dma_start(b_raw[:], b.rearrange("(p j) n -> p j n", j=PACK))
-        bias_sb = staged("bias_sb", [P, N // P], F32, BIAS_AT)
-        with nc.allow_non_contiguous_dma(reason="one bias value a partition"):
-            nc.sync.dma_start(bias_sb[:], bias.rearrange("(u p) -> p u", p=P))
 
         h_codes, h_plane = [], []
         h_rows, h_mix = [], []
@@ -205,9 +192,9 @@ def tile_list_adapter_moderation_probs_kernel(tc, tab, offs, w0_words, w0_scales
         b_codes = sb("b_codes", [P, N], U32)
         b_plane = sb("b_plane", [P, N], U8)
 
-        def base(acc, u, lo, hi):
+        def base(acc, u, lo, hi, passes):
             hf, c = divmod(lo, HALF)
-            for g in range(PASSES):
+            for g in passes:
                 nc.tensor.matmul_mx(
                     out=acc[:, : hi - lo],
                     lhsT=w0_sb[:, g, 2 * P * u : 2 * P * (u + 1)].bitcast(FP4X4),
@@ -233,12 +220,20 @@ def tile_list_adapter_moderation_probs_kernel(tc, tab, offs, w0_words, w0_scales
             nc.scalar.activation(prob[:], acc[:, : hi - lo], ACT.Sigmoid, bias=bias_sb[:, u : u + 1])
             nc.sync.dma_start(out[P * u : P * (u + 1), lo:hi], prob[:])
 
-        down_pass(0)
         gather_words(1)
+        lam_sb = staged("lam_sb", [P, PACK], F32, LAM_AT)
+        nc.sync.dma_start(lam_sb[:], lam.rearrange("(p t) -> p t", t=PACK))
+        b_raw = staged("b_raw", [P, PACK, N], F32, B_AT)
+        nc.sync.dma_start(b_raw[:], b.rearrange("(p j) n -> p j n", j=PACK))
+        bias_sb = staged("bias_sb", [P, N // P], F32, BIAS_AT)
+        with nc.allow_non_contiguous_dma(reason="one bias value a partition"):
+            nc.sync.dma_start(bias_sb[:], bias.rearrange("(u p) -> p u", p=P))
+
         y_first = [bank(f"y_first{u}", 6 + u) for u in range(2)]
-        for u in range(2):
-            base(y_first[u], u, 0, HALF)
-        for g, split, parts in ((1, 80, 1), (2, 64, 1), (3, 44, 2)):
+        for g in (0, 2, 1, 3):
+            for u in range(2):
+                base(y_first[u], u, 0, HALF, (g,))
+        for g, split, parts in ((0, 96, 2), (1, 48, 2), (2, 48, 2), (3, 44, 4)):
             cast_a(g, 0, split, False)
             cast_a(g, split, P, True)
             quant_a(g, parts)
@@ -267,6 +262,5 @@ def tile_list_adapter_moderation_probs_kernel(tc, tab, offs, w0_words, w0_scales
             quant_h(1, 256 * c, 256 * (c + 1))
             y_rest = [bank(f"y_rest{c}_{u}", 2 + 2 * c + u) for u in range(2)]
             for u in range(2):
-                base(y_rest[u], u, lo, lo + 256)
-            for u in range(2):
+                base(y_rest[u], u, lo, lo + 256, range(PASSES))
                 up(y_rest[u], u, lo, lo + 256)

@@ -37,68 +37,76 @@ def tile_list_adapter_moderation_probs_kernel(tc, tab, offs, w0_words, w0_scales
 
         stage = ctx.enter_context(tc.tile_pool(name="stage", bufs=1))
         KB = 1024
-        A_AT = [0, 10 * KB, 24 * KB, 32 * KB]
-        PICKED_AT = [7 * KB, 19 * KB]
-        B_AT = 18 * KB
-        LAM_AT = 22 * KB
-        BIAS_AT = 22 * KB + 64
-        WORDS_AT = [24 * KB, 40 * KB]
+        WORDS_AT = [0, 16 * KB]
+        PICKED_SCALES_AT = WORDS_AT[0]
+        ROUNDED_AT = WORDS_AT[1]
+        SCALE_WIN_AT = 32 * KB
+        A_CODES0_AT = SCALE_WIN_AT
+        PICKED_AT = {(0, 0): 42 * KB, (0, 1): 44 * KB, (1, 0): 34 * KB, (1, 1): 36 * KB}
+        LAM_AT = 36 * KB
+        BIAS_AT = 36 * KB + 64
+        B_AT = 37 * KB
 
         def staged(name, shape, dtype, at):
             return stage.tile(shape, dtype, name=name, align_bytes=64, offset=at)
 
-        words_win = [staged(f"words_win{m}", [P, T], I32, WORDS_AT[m]) for m in range(2)]
-        scale_win = [words_win[1][:, T // 2 + m * T // 4 : T // 2 + (m + 1) * T // 4] for m in range(2)]
+        scale_win = staged("scale_win", [P, T // 4], I32, SCALE_WIN_AT)
+        nc.vector.memset(scale_win[:], 0)
         for m in range(2):
-            nc.sync.dma_start(
-                scale_win[m][96:P, :], tab[m, 512 * T :].rearrange("(q t) -> q t", t=T).bitcast(I32)
-            )
+            rows = tab[m, 512 * T :].rearrange("(h q r t) -> r q h t", h=2, q=4, r=4)
+            for r in range(4):
+                nc.gpsimd.dma_start(scale_win[8 * m + r : P : 16, :], rows[r].bitcast(I32))
         w0_plane = sb("w0_plane", [P, PASSES, N], U8)
-        nc.gpsimd.memset(w0_plane[:].rearrange("p a n -> p (a n)").bitcast(I32), 0)
+        nc.vector.memset(w0_plane[:].rearrange("p a n -> p (a n)").bitcast(I32), 0)
+        for r in range(4):
+            nc.gpsimd.dma_start(
+                w0_plane[r : P : 32, :, :].bitcast(I32),
+                w0_scales.rearrange("a (q r) n -> r q a n", r=4)[r].bitcast(I32),
+            )
+        shifted = {g: sb(f"v_plane{g}", [P, S], U8) for g in range(1, PASSES)}
+        for g in range(1, PASSES):
+            nc.vector.memset(shifted[g][96:P, :].bitcast(I32), 0)
         warm = sb("warm", [P, 2], F32)
         nc.vector.memset(warm[:, 0:1], 0.0)
-        for m in range(2):
-            nc.vector.memset(scale_win[m][0:96, :], 0)
-        v_plane = [sb(f"v_plane{h}", [P, 2, S], U8) for h in range(2)]
-        for h in range(2):
-            nc.gpsimd.memset(v_plane[h][:].rearrange("p m s -> p (m s)").bitcast(I32), 0)
-
-        for q in range(4):
-            nc.gpsimd.dma_start(
-                w0_plane[32 * q : 32 * q + 4, :, :].bitcast(I32),
-                w0_scales[:, 4 * q : 4 * q + 4, :].rearrange("a r n -> r a n").bitcast(I32),
-            )
         nc.scalar.activation(warm[:, 1:2], warm[:, 0:1], ACT.Sigmoid)
 
-        a_raw = {}
+        a_raw = [sb(f"a_raw{g}", [P, PACK, R], F32) for g in range(PASSES)]
+        words_win = [staged(f"words_win{m}", [P, T], I32, WORDS_AT[m]) for m in range(2)]
+        w0_sb = sb("w0_sb", [P, PASSES, 2 * N], U8)
 
         def load_a(g):
-            raw = staged(f"a_raw{g}", [P, PACK, R], F32, A_AT[g])
-            nc.sync.dma_start(raw[:], a[512 * g : 512 * (g + 1), :].rearrange("(p j) r -> p j r", j=PACK))
-            a_raw[g] = raw
+            nc.sync.dma_start(a_raw[g][:], a[512 * g : 512 * (g + 1), :].rearrange("(p j) r -> p j r", j=PACK))
 
-        def load_words(m, lo, hi):
-            words = tab[m, : 512 * T].rearrange("(p c) -> p c", p=P).bitcast(I32)
-            nc.sync.dma_start(words_win[m][:, lo:hi], words[:, lo:hi])
+        def load_words(m):
+            nc.sync.dma_start(words_win[m][:], tab[m, : 512 * T].rearrange("(p c) -> p c", p=P).bitcast(I32))
 
-        load_words(0, 0, T)
-        w0_sb = sb("w0_sb", [P, PASSES, 2 * N], U8)
+        load_words(0)
+        load_a(0)
         nc.sync.dma_start(w0_sb[:].bitcast(I32), w0_words.rearrange("a p c -> p a c").bitcast(I32))
-        load_words(1, 0, T // 2)
+        load_words(1)
+        for g in range(1, PASSES):
+            load_a(g)
 
-        a_bf = [sb(f"a_bf{g}", [P, PACK, P, PACK], BF16) for g in range(PASSES)]
-        a_codes = [sb(f"a_codes{g}", [P, R], U32) for g in range(PASSES)]
-        a_plane = [sb(f"a_plane{g}", [P, R], U8) for g in range(PASSES)]
+        a_bf, a_codes, a_plane = {}, {}, {}
 
-        def cast_a(g, lo, hi, on_vector):
-            dst = a_bf[g][:, :, lo:hi, :].rearrange("p t m j -> p m j t")
-            src = a_raw[g][:, :, 4 * lo : 4 * hi].rearrange("p j (m t) -> p m j t", t=PACK)
-            if on_vector:
-                nc.vector.tensor_copy(dst, src)
+        def cast_a(g, split):
+            if g == 0:
+                a_bf[g] = sb("a_bf0", [P, PACK, P, PACK], BF16)
             else:
-                nc.scalar.copy(dst, src)
+                a_bf[g] = staged(f"a_bf{g}", [P, PACK, P, PACK], BF16, ROUNDED_AT)
+            for lo, hi, copy in ((0, split, nc.scalar.copy), (split, P, nc.vector.tensor_copy)):
+                if lo < hi:
+                    copy(
+                        a_bf[g][:, :, lo:hi, :].rearrange("p t m j -> p m j t"),
+                        a_raw[g][:, :, 4 * lo : 4 * hi].rearrange("p j (m t) -> p m j t", t=PACK),
+                    )
 
         def quant_a(g, parts):
+            if g == 0:
+                a_codes[g] = staged("a_codes0", [P, R], U32, A_CODES0_AT)
+            else:
+                a_codes[g] = sb(f"a_codes{g}", [P, R], U32)
+            a_plane[g] = sb(f"a_plane{g}", [P, R], U8)
             flat = a_bf[g][:].rearrange("p t m j -> p (t m j)")
             w = R // parts
             for i in range(parts):
@@ -112,7 +120,7 @@ def tile_list_adapter_moderation_probs_kernel(tc, tab, offs, w0_words, w0_scales
 
         def gather_words(m):
             for hf in range(HALVES):
-                g = staged(f"picked{m}_{hf}", [P, HALF], I32, PICKED_AT[m] + 2 * KB * hf)
+                g = staged(f"picked{m}_{hf}", [P, HALF], I32, PICKED_AT[m, hf])
                 nc.vector.tensor_copy(
                     g[:].bitcast(U32), words_win[m][:].bitcast(U32).indirect(offsets[:, 32 * hf : 32 * (hf + 1)])
                 )
@@ -136,7 +144,7 @@ def tile_list_adapter_moderation_probs_kernel(tc, tab, offs, w0_words, w0_scales
                 lhsT=a_codes[g][:, P * t : P * (t + 1)].bitcast(FP8X4),
                 lhsT_scale=a_plane[g][:, P * t : P * (t + 1)],
                 rhs=v_words[g, hf].bitcast(FP4X4),
-                rhs_scale=v_plane[g % 2][:, g // 2, HALF * hf : HALF * (hf + 1)],
+                rhs_scale=v_plane[g][:, HALF * hf : HALF * (hf + 1)],
                 start=(g == 0),
                 stop=(g == PASSES - 1),
             )
@@ -145,23 +153,16 @@ def tile_list_adapter_moderation_probs_kernel(tc, tab, offs, w0_words, w0_scales
             for hf, t in early:
                 down(g, hf, t)
 
-        picked_scales = sb("picked_scales", [P, 2, S], U8)
-        for m in range(2):
-            nc.vector.tensor_copy(picked_scales[:, m, :], scale_win[m].bitcast(U8).indirect(offsets[:]))
-        for move in range(8):
-            h, q = divmod(move, 4)
-            if move == 3:
-                load_words(1, T // 2, T)
-            first = 96 + 16 * h + 4 * q
-            nc.sync.dma_start(
-                v_plane[h][32 * q : 32 * q + 4, :, :].rearrange("p m s -> p (m s)").bitcast(I32),
-                picked_scales[first : first + 4, :, :].rearrange("p m s -> p (m s)").bitcast(I32),
-            )
+        cast_a(0, P)
         gather_words(0)
-        load_a(0)
-        load_a(1)
-        load_a(2)
-        load_a(3)
+        picked_scales = staged("picked_scales", [P, S], U8, PICKED_SCALES_AT)
+        nc.vector.tensor_copy(picked_scales[:], scale_win[:].bitcast(U8).indirect(offsets[:]))
+        v_plane = {0: picked_scales}
+        for g in range(1, PASSES):
+            up_by = 16 * (g % 2) + 8 * (g // 2)
+            nc.scalar.dma_start(shifted[g][0 : P - up_by, :].bitcast(I32), picked_scales[up_by:P, :].bitcast(I32))
+            v_plane[g] = shifted[g]
+        quant_a(0, 2)
 
         h_codes, h_plane = [], []
         h_rows, h_mix = [], []
@@ -188,7 +189,6 @@ def tile_list_adapter_moderation_probs_kernel(tc, tab, offs, w0_words, w0_scales
                 in_=h_mix[hf][:, lo:hi, :].rearrange("p n t -> p (n t)"),
             )
 
-        b_bf = sb("b_bf", [P, N, PACK], BF16)
         b_codes = sb("b_codes", [P, N], U32)
         b_plane = sb("b_plane", [P, N], U8)
 
@@ -200,7 +200,7 @@ def tile_list_adapter_moderation_probs_kernel(tc, tab, offs, w0_words, w0_scales
                     lhsT=w0_sb[:, g, 2 * P * u : 2 * P * (u + 1)].bitcast(FP4X4),
                     lhsT_scale=w0_plane[:, g, P * u : P * (u + 1)],
                     rhs=v_words[g, hf][:, c : c + hi - lo].bitcast(FP4X4),
-                    rhs_scale=v_plane[g % 2][:, g // 2, lo:hi],
+                    rhs_scale=v_plane[g][:, lo:hi],
                     start=(g == 0),
                     stop=False,
                 )
@@ -230,15 +230,16 @@ def tile_list_adapter_moderation_probs_kernel(tc, tab, offs, w0_words, w0_scales
             nc.sync.dma_start(bias_sb[:], bias.rearrange("(u p) -> p u", p=P))
 
         y_first = [bank(f"y_first{u}", 6 + u) for u in range(2)]
-        for g in (0, 2, 1, 3):
+        down_pass(0)
+        for g in range(PASSES):
             for u in range(2):
                 base(y_first[u], u, 0, HALF, (g,))
-        for g, split, parts in ((0, 96, 2), (1, 48, 2), (2, 48, 2), (3, 44, 4)):
-            cast_a(g, 0, split, False)
-            cast_a(g, split, P, True)
+        for g, split, parts in ((1, 64, 2), (2, 48, 2), (3, 44, 4)):
+            cast_a(g, split)
             quant_a(g, parts)
             down_pass(g)
 
+        b_bf = staged("b_bf", [P, N, PACK], BF16, ROUNDED_AT)
         nc.vector.tensor_copy(
             b_bf[:].rearrange("p (c i) j -> p c j i", i=4), b_raw[:].rearrange("p j (c i) -> p c j i", i=4)
         )

@@ -39,13 +39,14 @@ def tile_list_adapter_moderation_probs_kernel(tc, tab, offs, w0_words, w0_scales
         KB = 1024
         WORDS_AT = [0, 16 * KB]
         PICKED_SCALES_AT = WORDS_AT[0]
-        ROUNDED_AT = WORDS_AT[1]
-        SCALE_WIN_AT = 32 * KB
-        A_CODES0_AT = SCALE_WIN_AT
-        PICKED_AT = {(0, 0): 42 * KB, (0, 1): 44 * KB, (1, 0): 34 * KB, (1, 1): 36 * KB}
-        LAM_AT = 36 * KB
-        BIAS_AT = 36 * KB + 64
-        B_AT = 37 * KB
+        A_BF_AT = {2: WORDS_AT[1] + 2 * KB, 3: WORDS_AT[1] + 6 * KB}
+        SCALE_WIN_AT = 40 * KB
+        A_RAW_AT = {2: SCALE_WIN_AT + 64 - 8 * KB, 3: SCALE_WIN_AT + 4 * KB - 64}
+        A_PLANE1_AT = SCALE_WIN_AT + 64
+        PICKED_AT = {(0, 0): WORDS_AT[1], (0, 1): 52 * KB, (1, 0): SCALE_WIN_AT + KB, (1, 1): 54 * KB}
+        LAM_AT = 54 * KB
+        BIAS_AT = 54 * KB + 64
+        B_AT = 55 * KB
 
         def staged(name, shape, dtype, at):
             return stage.tile(shape, dtype, name=name, align_bytes=64, offset=at)
@@ -70,30 +71,32 @@ def tile_list_adapter_moderation_probs_kernel(tc, tab, offs, w0_words, w0_scales
         nc.vector.memset(warm[:, 0:1], 0.0)
         nc.scalar.activation(warm[:, 1:2], warm[:, 0:1], ACT.Sigmoid)
 
-        a_raw = [sb(f"a_raw{g}", [P, PACK, R], F32) for g in range(PASSES)]
-        words_win = [staged(f"words_win{m}", [P, T], I32, WORDS_AT[m]) for m in range(2)]
+        a_raw, words_win = {}, {}
         w0_sb = sb("w0_sb", [P, PASSES, 2 * N], U8)
 
         def load_a(g):
+            if g in A_RAW_AT:
+                a_raw[g] = staged(f"a_raw{g}", [P, PACK, R], F32, A_RAW_AT[g])
+            else:
+                a_raw[g] = sb(f"a_raw{g}", [P, PACK, R], F32)
             nc.sync.dma_start(a_raw[g][:], a[512 * g : 512 * (g + 1), :].rearrange("(p j) r -> p j r", j=PACK))
 
         def load_words(m):
+            words_win[m] = staged(f"words_win{m}", [P, T], I32, WORDS_AT[m])
             nc.sync.dma_start(words_win[m][:], tab[m, : 512 * T].rearrange("(p c) -> p c", p=P).bitcast(I32))
 
-        load_words(0)
         load_a(0)
+        load_words(0)
         nc.sync.dma_start(w0_sb[:].bitcast(I32), w0_words.rearrange("a p c -> p a c").bitcast(I32))
-        load_words(1)
-        for g in range(1, PASSES):
-            load_a(g)
+        load_a(1)
 
         a_bf, a_codes, a_plane = {}, {}, {}
 
         def cast_a(g, split):
-            if g == 0:
-                a_bf[g] = sb("a_bf0", [P, PACK, P, PACK], BF16)
+            if g in A_BF_AT:
+                a_bf[g] = staged(f"a_bf{g}", [P, PACK, P, PACK], BF16, A_BF_AT[g])
             else:
-                a_bf[g] = staged(f"a_bf{g}", [P, PACK, P, PACK], BF16, ROUNDED_AT)
+                a_bf[g] = sb(f"a_bf{g}", [P, PACK, P, PACK], BF16)
             for lo, hi, copy in ((0, split, nc.scalar.copy), (split, P, nc.vector.tensor_copy)):
                 if lo < hi:
                     copy(
@@ -102,11 +105,11 @@ def tile_list_adapter_moderation_probs_kernel(tc, tab, offs, w0_words, w0_scales
                     )
 
         def quant_a(g, parts):
-            if g == 0:
-                a_codes[g] = staged("a_codes0", [P, R], U32, A_CODES0_AT)
+            a_codes[g] = sb(f"a_codes{g}", [P, R], U32)
+            if g == 1:
+                a_plane[g] = staged("a_plane1", [P, R], U8, A_PLANE1_AT)
             else:
-                a_codes[g] = sb(f"a_codes{g}", [P, R], U32)
-            a_plane[g] = sb(f"a_plane{g}", [P, R], U8)
+                a_plane[g] = sb(f"a_plane{g}", [P, R], U8)
             flat = a_bf[g][:].rearrange("p t m j -> p (t m j)")
             w = R // parts
             for i in range(parts):
@@ -154,15 +157,20 @@ def tile_list_adapter_moderation_probs_kernel(tc, tab, offs, w0_words, w0_scales
                 down(g, hf, t)
 
         cast_a(0, P)
+        quant_a(0, 1)
         gather_words(0)
+        load_words(1)
         picked_scales = staged("picked_scales", [P, S], U8, PICKED_SCALES_AT)
         nc.vector.tensor_copy(picked_scales[:], scale_win[:].bitcast(U8).indirect(offsets[:]))
         v_plane = {0: picked_scales}
         for g in range(1, PASSES):
             up_by = 16 * (g % 2) + 8 * (g // 2)
-            nc.scalar.dma_start(shifted[g][0 : P - up_by, :].bitcast(I32), picked_scales[up_by:P, :].bitcast(I32))
+            nc.sync.dma_start(shifted[g][0 : P - up_by, :].bitcast(I32), picked_scales[up_by:P, :].bitcast(I32))
             v_plane[g] = shifted[g]
-        quant_a(0, 2)
+        load_a(2)
+        load_a(3)
+        cast_a(1, P)
+        quant_a(1, 1)
 
         h_codes, h_plane = [], []
         h_rows, h_mix = [], []
@@ -230,16 +238,17 @@ def tile_list_adapter_moderation_probs_kernel(tc, tab, offs, w0_words, w0_scales
             nc.sync.dma_start(bias_sb[:], bias.rearrange("(u p) -> p u", p=P))
 
         y_first = [bank(f"y_first{u}", 6 + u) for u in range(2)]
-        down_pass(0)
         for g in range(PASSES):
+            if g < 2:
+                down_pass(g)
             for u in range(2):
                 base(y_first[u], u, 0, HALF, (g,))
-        for g, split, parts in ((1, 64, 2), (2, 48, 2), (3, 44, 4)):
+        for g, split, parts in ((2, 64, 2), (3, 44, 4)):
             cast_a(g, split)
             quant_a(g, parts)
             down_pass(g)
 
-        b_bf = staged("b_bf", [P, N, PACK], BF16, ROUNDED_AT)
+        b_bf = sb("b_bf", [P, N, PACK], BF16)
         nc.vector.tensor_copy(
             b_bf[:].rearrange("p (c i) j -> p c j i", i=4), b_raw[:].rearrange("p j (c i) -> p c j i", i=4)
         )

@@ -38,41 +38,40 @@ def tile_list_adapter_moderation_probs_kernel(tc, tab, offs, w0_words, w0_scales
         stage = ctx.enter_context(tc.tile_pool(name="stage", bufs=1))
         KB = 1024
         WORDS_AT = [0, 16 * KB]
-        PICKED_SCALES_AT = WORDS_AT[0]
-        A_BF_AT = {2: WORDS_AT[1] + 2 * KB, 3: WORDS_AT[1] + 6 * KB}
-        SCALE_WIN_AT = 40 * KB
-        A_RAW_AT = {2: SCALE_WIN_AT + 64 - 8 * KB, 3: SCALE_WIN_AT + 4 * KB - 64}
-        A_PLANE1_AT = SCALE_WIN_AT + 64
-        PICKED_AT = {(0, 0): WORDS_AT[1], (0, 1): 52 * KB, (1, 0): SCALE_WIN_AT + KB, (1, 1): 54 * KB}
-        LAM_AT = 54 * KB
-        BIAS_AT = 54 * KB + 64
-        B_AT = 55 * KB
+        W0_AT = 32 * KB
+        A_RAW_AT = {0: 34 * KB, 1: 42 * KB, 2: 50 * KB, 3: 58 * KB}
+        SCALE_WIN_AT = [66 * KB, 34 * KB - 64]
+        A_BF_AT = {}
+        PICKED_AT = {(0, 0): 49 * KB, (0, 1): 60 * KB, (1, 0): 76 * KB, (1, 1): 70 * KB}
+        LAM_AT = 70 * KB
+        BIAS_AT = 70 * KB + 64
+        B_AT = 71 * KB
 
         def staged(name, shape, dtype, at):
             return stage.tile(shape, dtype, name=name, align_bytes=64, offset=at)
 
-        scale_win = staged("scale_win", [P, T // 4], I32, SCALE_WIN_AT)
-        nc.vector.memset(scale_win[:], 0)
+        scale_win = [staged(f"scale_win{m}", [P, T // 4], I32, SCALE_WIN_AT[m]) for m in range(2)]
         for m in range(2):
-            rows = tab[m, 512 * T :].rearrange("(h q r t) -> r q h t", h=2, q=4, r=4)
-            for r in range(4):
-                nc.gpsimd.dma_start(scale_win[8 * m + r : P : 16, :], rows[r].bitcast(I32))
+            nc.sync.dma_start(
+                scale_win[m][96:P, :], tab[m, 512 * T :].rearrange("(q t) -> q t", t=T).bitcast(I32)
+            )
+        for m in range(2):
+            nc.vector.memset(scale_win[m][0:96, :], 0)
         w0_plane = sb("w0_plane", [P, PASSES, N], U8)
-        nc.vector.memset(w0_plane[:].rearrange("p a n -> p (a n)").bitcast(I32), 0)
+        nc.gpsimd.memset(w0_plane[:].rearrange("p a n -> p (a n)").bitcast(I32), 0)
+        planes = [sb(f"v_plane{h}", [P, 2, S], U8) for h in range(2)]
+        for h in range(2):
+            nc.gpsimd.memset(planes[h][:].rearrange("p m s -> p (m s)").bitcast(I32), 0)
         for r in range(4):
             nc.gpsimd.dma_start(
                 w0_plane[r : P : 32, :, :].bitcast(I32),
                 w0_scales.rearrange("a (q r) n -> r q a n", r=4)[r].bitcast(I32),
             )
-        shifted = {g: sb(f"v_plane{g}", [P, S], U8) for g in range(1, PASSES)}
-        for g in range(1, PASSES):
-            nc.vector.memset(shifted[g][96:P, :].bitcast(I32), 0)
         warm = sb("warm", [P, 2], F32)
         nc.vector.memset(warm[:, 0:1], 0.0)
         nc.scalar.activation(warm[:, 1:2], warm[:, 0:1], ACT.Sigmoid)
 
         a_raw, words_win = {}, {}
-        w0_sb = sb("w0_sb", [P, PASSES, 2 * N], U8)
 
         def load_a(g):
             if g in A_RAW_AT:
@@ -85,10 +84,8 @@ def tile_list_adapter_moderation_probs_kernel(tc, tab, offs, w0_words, w0_scales
             words_win[m] = staged(f"words_win{m}", [P, T], I32, WORDS_AT[m])
             nc.sync.dma_start(words_win[m][:], tab[m, : 512 * T].rearrange("(p c) -> p c", p=P).bitcast(I32))
 
-        load_a(0)
         load_words(0)
-        nc.sync.dma_start(w0_sb[:].bitcast(I32), w0_words.rearrange("a p c -> p a c").bitcast(I32))
-        load_a(1)
+        load_words(1)
 
         a_bf, a_codes, a_plane = {}, {}, {}
 
@@ -106,10 +103,7 @@ def tile_list_adapter_moderation_probs_kernel(tc, tab, offs, w0_words, w0_scales
 
         def quant_a(g, parts):
             a_codes[g] = sb(f"a_codes{g}", [P, R], U32)
-            if g == 1:
-                a_plane[g] = staged("a_plane1", [P, R], U8, A_PLANE1_AT)
-            else:
-                a_plane[g] = sb(f"a_plane{g}", [P, R], U8)
+            a_plane[g] = sb(f"a_plane{g}", [P, R], U8)
             flat = a_bf[g][:].rearrange("p t m j -> p (t m j)")
             w = R // parts
             for i in range(parts):
@@ -156,21 +150,23 @@ def tile_list_adapter_moderation_probs_kernel(tc, tab, offs, w0_words, w0_scales
             for hf, t in early:
                 down(g, hf, t)
 
-        cast_a(0, P)
-        quant_a(0, 1)
+        picked_scales = sb("picked_scales", [P, 2, S], U8)
+        for m in range(2):
+            nc.vector.tensor_copy(picked_scales[:, m, :], scale_win[m][:].bitcast(U8).indirect(offsets[:]))
+        for h in range(2):
+            for r in range(4):
+                first = 96 + 16 * h + r
+                nc.sync.dma_start(
+                    planes[h][r : P : 32, :, :].rearrange("p m s -> p (m s)").bitcast(I32),
+                    picked_scales[first : first + 13 : 4, :, :].rearrange("p m s -> p (m s)").bitcast(I32),
+                )
+        v_plane = {g: planes[g % 2][:, g // 2, :] for g in range(PASSES)}
+        w0_sb = staged("w0_sb", [P, PASSES, 2 * N], U8, W0_AT)
+        nc.sync.dma_start(w0_sb[:].bitcast(I32), w0_words.rearrange("a p c -> p a c").bitcast(I32))
+        load_a(0)
         gather_words(0)
-        load_words(1)
-        picked_scales = staged("picked_scales", [P, S], U8, PICKED_SCALES_AT)
-        nc.vector.tensor_copy(picked_scales[:], scale_win[:].bitcast(U8).indirect(offsets[:]))
-        v_plane = {0: picked_scales}
         for g in range(1, PASSES):
-            up_by = 16 * (g % 2) + 8 * (g // 2)
-            nc.sync.dma_start(shifted[g][0 : P - up_by, :].bitcast(I32), picked_scales[up_by:P, :].bitcast(I32))
-            v_plane[g] = shifted[g]
-        load_a(2)
-        load_a(3)
-        cast_a(1, P)
-        quant_a(1, 1)
+            load_a(g)
 
         h_codes, h_plane = [], []
         h_rows, h_mix = [], []
@@ -239,11 +235,9 @@ def tile_list_adapter_moderation_probs_kernel(tc, tab, offs, w0_words, w0_scales
 
         y_first = [bank(f"y_first{u}", 6 + u) for u in range(2)]
         for g in range(PASSES):
-            if g < 2:
-                down_pass(g)
             for u in range(2):
                 base(y_first[u], u, 0, HALF, (g,))
-        for g, split, parts in ((2, 64, 2), (3, 44, 4)):
+        for g, split, parts in ((0, 48, 2), (1, 48, 2), (2, 48, 2), (3, 44, 4)):
             cast_a(g, split)
             quant_a(g, parts)
             down_pass(g)

@@ -33,7 +33,6 @@ def tile_list_adapter_moderation_probs_kernel(tc, tab, offs, w0_words, w0_scales
             return keep.tile(shape, dtype, name=name, align_bytes=64)
 
         offsets = sb("offsets", [P, S // 16], U16)
-        nc.sync.dma_start(offsets[:], offs)
 
         stage = ctx.enter_context(tc.tile_pool(name="stage", bufs=1))
         KB = 1024
@@ -41,9 +40,7 @@ def tile_list_adapter_moderation_probs_kernel(tc, tab, offs, w0_words, w0_scales
         W0_AT = 32 * KB
         A_RAW_AT = {0: 34 * KB, 1: 42 * KB, 2: 50 * KB, 3: 58 * KB}
         SCALE_WIN_AT = [66 * KB, 34 * KB - 64]
-        A_BF_AT = {}
-        PICKED_AT = {(0, 0): 49 * KB, (0, 1): 60 * KB, (1, 0): 76 * KB, (1, 1): 70 * KB}
-        LAM_AT = 70 * KB
+        PICKED_AT = {(0, 0): 49 * KB, (0, 1): 61 * KB, (1, 0): 76 * KB, (1, 1): 70 * KB}
         BIAS_AT = 70 * KB + 64
         B_AT = 71 * KB
 
@@ -55,6 +52,8 @@ def tile_list_adapter_moderation_probs_kernel(tc, tab, offs, w0_words, w0_scales
             nc.sync.dma_start(
                 scale_win[m][96:P, :], tab[m, 512 * T :].rearrange("(q t) -> q t", t=T).bitcast(I32)
             )
+            if m == 0:
+                nc.sync.dma_start(offsets[:], offs)
         for m in range(2):
             nc.vector.memset(scale_win[m][0:96, :], 0)
         w0_plane = sb("w0_plane", [P, PASSES, N], U8)
@@ -74,11 +73,14 @@ def tile_list_adapter_moderation_probs_kernel(tc, tab, offs, w0_words, w0_scales
         a_raw, words_win = {}, {}
 
         def load_a(g):
-            if g in A_RAW_AT:
+            rows = a[512 * g : 512 * (g + 1), :].rearrange("(p j) r -> p j r", j=PACK)
+            if g < PASSES - 1:
                 a_raw[g] = staged(f"a_raw{g}", [P, PACK, R], F32, A_RAW_AT[g])
-            else:
-                a_raw[g] = sb(f"a_raw{g}", [P, PACK, R], F32)
-            nc.sync.dma_start(a_raw[g][:], a[512 * g : 512 * (g + 1), :].rearrange("(p j) r -> p j r", j=PACK))
+                nc.sync.dma_start(a_raw[g][:], rows)
+                return
+            for e in range(2):
+                a_raw[g, e] = staged(f"a_raw{g}_{e}", [P, 2, R], F32, A_RAW_AT[g] + 4 * KB * e)
+                nc.sync.dma_start(a_raw[g, e][:], rows[:, 2 * e : 2 * e + 2, :])
 
         def load_words(m):
             words_win[m] = staged(f"words_win{m}", [P, T], I32, WORDS_AT[m])
@@ -86,20 +88,16 @@ def tile_list_adapter_moderation_probs_kernel(tc, tab, offs, w0_words, w0_scales
 
         load_words(0)
         load_words(1)
+        lam_sb = sb("lam_sb", [P, PACK], F32)
+        nc.sync.dma_start(lam_sb[:], lam.rearrange("(p t) -> p t", t=PACK))
 
-        a_bf, a_codes, a_plane = {}, {}, {}
+        a_bf = [sb(f"a_bf{g}", [P, PACK, P, PACK], BF16) for g in range(PASSES)]
+        a_codes, a_plane = {}, {}
 
-        def cast_a(g, split):
-            if g in A_BF_AT:
-                a_bf[g] = staged(f"a_bf{g}", [P, PACK, P, PACK], BF16, A_BF_AT[g])
-            else:
-                a_bf[g] = sb(f"a_bf{g}", [P, PACK, P, PACK], BF16)
-            for lo, hi, copy in ((0, split, nc.scalar.copy), (split, P, nc.vector.tensor_copy)):
-                if lo < hi:
-                    copy(
-                        a_bf[g][:, :, lo:hi, :].rearrange("p t m j -> p m j t"),
-                        a_raw[g][:, :, 4 * lo : 4 * hi].rearrange("p j (m t) -> p m j t", t=PACK),
-                    )
+        def cast_rows(g, raw, lo_j, hi_j):
+            src = raw[:].rearrange("p j (m t) -> p m j t", t=PACK)
+            for lo, copy in ((0, nc.vector.tensor_copy), (2, nc.scalar.copy)):
+                copy(a_bf[g][:, lo : lo + 2, :, lo_j:hi_j].rearrange("p t m j -> p m j t"), src[:, :, :, lo : lo + 2])
 
         def quant_a(g, parts):
             a_codes[g] = sb(f"a_codes{g}", [P, R], U32)
@@ -153,17 +151,20 @@ def tile_list_adapter_moderation_probs_kernel(tc, tab, offs, w0_words, w0_scales
         picked_scales = sb("picked_scales", [P, 2, S], U8)
         for m in range(2):
             nc.vector.tensor_copy(picked_scales[:, m, :], scale_win[m][:].bitcast(U8).indirect(offsets[:]))
-        for h in range(2):
+        def move_planes(h):
             for r in range(4):
                 first = 96 + 16 * h + r
                 nc.sync.dma_start(
                     planes[h][r : P : 32, :, :].rearrange("p m s -> p (m s)").bitcast(I32),
                     picked_scales[first : first + 13 : 4, :, :].rearrange("p m s -> p (m s)").bitcast(I32),
                 )
+
         v_plane = {g: planes[g % 2][:, g // 2, :] for g in range(PASSES)}
+        move_planes(0)
         w0_sb = staged("w0_sb", [P, PASSES, 2 * N], U8, W0_AT)
         nc.sync.dma_start(w0_sb[:].bitcast(I32), w0_words.rearrange("a p c -> p a c").bitcast(I32))
         load_a(0)
+        move_planes(1)
         gather_words(0)
         for g in range(1, PASSES):
             load_a(g)
@@ -225,8 +226,6 @@ def tile_list_adapter_moderation_probs_kernel(tc, tab, offs, w0_words, w0_scales
             nc.sync.dma_start(out[P * u : P * (u + 1), lo:hi], prob[:])
 
         gather_words(1)
-        lam_sb = staged("lam_sb", [P, PACK], F32, LAM_AT)
-        nc.sync.dma_start(lam_sb[:], lam.rearrange("(p t) -> p t", t=PACK))
         b_raw = staged("b_raw", [P, PACK, N], F32, B_AT)
         nc.sync.dma_start(b_raw[:], b.rearrange("(p j) n -> p j n", j=PACK))
         bias_sb = staged("bias_sb", [P, N // P], F32, BIAS_AT)
@@ -234,13 +233,17 @@ def tile_list_adapter_moderation_probs_kernel(tc, tab, offs, w0_words, w0_scales
             nc.sync.dma_start(bias_sb[:], bias.rearrange("(u p) -> p u", p=P))
 
         y_first = [bank(f"y_first{u}", 6 + u) for u in range(2)]
-        for g in range(PASSES):
+        for g in (0, 2, 1, 3):
             for u in range(2):
                 base(y_first[u], u, 0, HALF, (g,))
-        for g, split, parts in ((0, 48, 2), (1, 48, 2), (2, 48, 2), (3, 44, 4)):
-            cast_a(g, split)
-            quant_a(g, parts)
+        for g in range(PASSES - 1):
+            cast_rows(g, a_raw[g], 0, PACK)
+            quant_a(g, 2)
             down_pass(g)
+        for e in range(2):
+            cast_rows(3, a_raw[3, e], 2 * e, 2 * e + 2)
+        quant_a(3, 4)
+        down_pass(3)
 
         b_bf = sb("b_bf", [P, N, PACK], BF16)
         nc.vector.tensor_copy(

@@ -37,9 +37,9 @@ def tile_list_adapter_moderation_probs_kernel(tc, tab, offs, w0_words, w0_scales
         stage = ctx.enter_context(tc.tile_pool(name="stage", bufs=1))
         KB = 1024
         WORDS_AT = [0, 16 * KB]
-        W0_AT = 32 * KB
+        SCALE_WIN_AT = WORDS_AT[1]
         A_RAW_AT = {0: 34 * KB, 1: 42 * KB, 2: 50 * KB, 3: 58 * KB}
-        SCALE_WIN_AT = [66 * KB, 34 * KB - 64]
+        PICKED_SCALES_AT = 34 * KB - 64
         PICKED_AT = {(0, 0): 49 * KB, (0, 1): 61 * KB, (1, 0): 76 * KB, (1, 1): 70 * KB}
         BIAS_AT = 70 * KB + 64
         B_AT = 71 * KB
@@ -47,15 +47,15 @@ def tile_list_adapter_moderation_probs_kernel(tc, tab, offs, w0_words, w0_scales
         def staged(name, shape, dtype, at):
             return stage.tile(shape, dtype, name=name, align_bytes=64, offset=at)
 
-        scale_win = [staged(f"scale_win{m}", [P, T // 4], I32, SCALE_WIN_AT[m]) for m in range(2)]
+        scale_win = staged("scale_win", [P, T // 4], I32, SCALE_WIN_AT)
         for m in range(2):
             nc.sync.dma_start(
-                scale_win[m][96:P, :], tab[m, 512 * T :].rearrange("(q t) -> q t", t=T).bitcast(I32)
+                scale_win[32 + 32 * m : 64 + 32 * m, :], tab[m, 512 * T :].rearrange("(q t) -> q t", t=T).bitcast(I32)
             )
             if m == 0:
                 nc.sync.dma_start(offsets[:], offs)
-        for m in range(2):
-            nc.vector.memset(scale_win[m][0:96, :], 0)
+        nc.vector.memset(scale_win[0:32, :], 0)
+        nc.vector.memset(scale_win[96:P, :], 0)
         w0_plane = sb("w0_plane", [P, PASSES, N], U8)
         nc.gpsimd.memset(w0_plane[:].rearrange("p a n -> p (a n)").bitcast(I32), 0)
         planes = [sb(f"v_plane{h}", [P, 2, S], U8) for h in range(2)]
@@ -87,7 +87,8 @@ def tile_list_adapter_moderation_probs_kernel(tc, tab, offs, w0_words, w0_scales
             nc.sync.dma_start(words_win[m][:], tab[m, : 512 * T].rearrange("(p c) -> p c", p=P).bitcast(I32))
 
         load_words(0)
-        load_words(1)
+        w0_sb = sb("w0_sb", [P, PASSES, 2 * N], U8)
+        nc.sync.dma_start(w0_sb[:].bitcast(I32), w0_words.rearrange("a p c -> p a c").bitcast(I32))
         lam_sb = sb("lam_sb", [P, PACK], F32)
         nc.sync.dma_start(lam_sb[:], lam.rearrange("(p t) -> p t", t=PACK))
 
@@ -96,7 +97,7 @@ def tile_list_adapter_moderation_probs_kernel(tc, tab, offs, w0_words, w0_scales
 
         def cast_rows(g, raw, lo_j, hi_j):
             src = raw[:].rearrange("p j (m t) -> p m j t", t=PACK)
-            for lo, copy in ((0, nc.vector.tensor_copy), (2, nc.scalar.copy)):
+            for lo, copy in ((0, nc.scalar.copy if g == 0 else nc.vector.tensor_copy), (2, nc.scalar.copy)):
                 copy(a_bf[g][:, lo : lo + 2, :, lo_j:hi_j].rearrange("p t m j -> p m j t"), src[:, :, :, lo : lo + 2])
 
         def quant_a(g, parts):
@@ -148,21 +149,23 @@ def tile_list_adapter_moderation_probs_kernel(tc, tab, offs, w0_words, w0_scales
             for hf, t in early:
                 down(g, hf, t)
 
-        picked_scales = sb("picked_scales", [P, 2, S], U8)
-        for m in range(2):
-            nc.vector.tensor_copy(picked_scales[:, m, :], scale_win[m][:].bitcast(U8).indirect(offsets[:]))
+        picked_scales = staged("picked_scales", [P, S], U8, PICKED_SCALES_AT)
+        nc.vector.tensor_copy(picked_scales[:], scale_win[:].bitcast(U8).indirect(offsets[:]))
+        stacked = sb("stacked", [P, 2, S // 4], I32)
+        nc.sync.dma_start(stacked[32:64, 1, :], picked_scales[64:96, :].bitcast(I32))
+        nc.vector.tensor_copy(stacked[32:64, 0, :], picked_scales[32:64, :].bitcast(I32))
+        load_words(1)
+
         def move_planes(h):
             for r in range(4):
-                first = 96 + 16 * h + r
+                first = 32 + 16 * h + r
                 nc.sync.dma_start(
                     planes[h][r : P : 32, :, :].rearrange("p m s -> p (m s)").bitcast(I32),
-                    picked_scales[first : first + 13 : 4, :, :].rearrange("p m s -> p (m s)").bitcast(I32),
+                    stacked[first : first + 13 : 4, :, :].rearrange("p m s -> p (m s)"),
                 )
 
         v_plane = {g: planes[g % 2][:, g // 2, :] for g in range(PASSES)}
         move_planes(0)
-        w0_sb = staged("w0_sb", [P, PASSES, 2 * N], U8, W0_AT)
-        nc.sync.dma_start(w0_sb[:].bitcast(I32), w0_words.rearrange("a p c -> p a c").bitcast(I32))
         load_a(0)
         move_planes(1)
         gather_words(0)

@@ -29,8 +29,8 @@ def tile_list_adapter_moderation_probs_kernel(tc, tab, offs, w0_words, w0_scales
         keep = ctx.enter_context(tc.tile_pool(name="keep", bufs=1))
         psum = ctx.enter_context(tc.psum_pool(name="psum", bufs=1))
 
-        def sb(name, shape, dtype):
-            return keep.tile(shape, dtype, name=name, align_bytes=64)
+        def sb(name, shape, dtype, align=64):
+            return keep.tile(shape, dtype, name=name, align_bytes=align)
 
         offsets = sb("offsets", [P, S // 16], U16)
 
@@ -39,13 +39,15 @@ def tile_list_adapter_moderation_probs_kernel(tc, tab, offs, w0_words, w0_scales
         WORDS_AT = [0, 16 * KB]
         SCALE_WIN_AT = WORDS_AT[1]
         A_RAW_AT = {0: 34 * KB, 1: 42 * KB, 2: 50 * KB, 3: 58 * KB}
-        PICKED_SCALES_AT = 34 * KB - 64
-        PICKED_AT = {(0, 0): 49 * KB, (0, 1): 61 * KB, (1, 0): 76 * KB, (1, 1): 70 * KB}
-        BIAS_AT = 70 * KB + 64
+        PICKED_SCALES_AT = A_RAW_AT[0]
+        PICKED_AT = {(0, 0): 49 * KB, (0, 1): 61 * KB, (1, 0): 70 * KB, (1, 1): 70 * KB}
+        STACKED_AT = 78 * KB
+        LAM_AT = 70 * KB
+        BIAS_AT = 70 * KB + 256
         B_AT = 71 * KB
 
         def staged(name, shape, dtype, at):
-            return stage.tile(shape, dtype, name=name, align_bytes=64, offset=at)
+            return stage.tile(shape, dtype, name=name, align_bytes=256, offset=at)
 
         scale_win = staged("scale_win", [P, T // 4], I32, SCALE_WIN_AT)
         for m in range(2):
@@ -89,10 +91,8 @@ def tile_list_adapter_moderation_probs_kernel(tc, tab, offs, w0_words, w0_scales
         load_words(0)
         w0_sb = sb("w0_sb", [P, PASSES, 2 * N], U8)
         nc.sync.dma_start(w0_sb[:].bitcast(I32), w0_words.rearrange("a p c -> p a c").bitcast(I32))
-        lam_sb = sb("lam_sb", [P, PACK], F32)
-        nc.sync.dma_start(lam_sb[:], lam.rearrange("(p t) -> p t", t=PACK))
 
-        a_bf = [sb(f"a_bf{g}", [P, PACK, P, PACK], BF16) for g in range(PASSES)]
+        a_bf = [sb(f"a_bf{g}", [P, PACK, P, PACK], BF16, 256) for g in range(PASSES)]
         a_codes, a_plane = {}, {}
 
         def cast_rows(g, raw, lo_j, hi_j):
@@ -101,7 +101,10 @@ def tile_list_adapter_moderation_probs_kernel(tc, tab, offs, w0_words, w0_scales
                 copy(a_bf[g][:, lo : lo + 2, :, lo_j:hi_j].rearrange("p t m j -> p m j t"), src[:, :, :, lo : lo + 2])
 
         def quant_a(g, parts):
-            a_codes[g] = sb(f"a_codes{g}", [P, R], U32)
+            if g == 0:
+                a_codes[g] = staged("a_codes0", [P, R], U32, STACKED_AT)
+            else:
+                a_codes[g] = sb(f"a_codes{g}", [P, R], U32)
             a_plane[g] = sb(f"a_plane{g}", [P, R], U8)
             flat = a_bf[g][:].rearrange("p t m j -> p (t m j)")
             w = R // parts
@@ -151,7 +154,7 @@ def tile_list_adapter_moderation_probs_kernel(tc, tab, offs, w0_words, w0_scales
 
         picked_scales = staged("picked_scales", [P, S], U8, PICKED_SCALES_AT)
         nc.vector.tensor_copy(picked_scales[:], scale_win[:].bitcast(U8).indirect(offsets[:]))
-        stacked = sb("stacked", [P, 2, S // 4], I32)
+        stacked = staged("stacked", [P, 2, S // 4], I32, STACKED_AT)
         nc.sync.dma_start(stacked[32:64, 1, :], picked_scales[64:96, :].bitcast(I32))
         nc.vector.tensor_copy(stacked[32:64, 0, :], picked_scales[32:64, :].bitcast(I32))
         load_words(1)
@@ -229,6 +232,8 @@ def tile_list_adapter_moderation_probs_kernel(tc, tab, offs, w0_words, w0_scales
             nc.sync.dma_start(out[P * u : P * (u + 1), lo:hi], prob[:])
 
         gather_words(1)
+        lam_sb = staged("lam_sb", [P, PACK], F32, LAM_AT)
+        nc.sync.dma_start(lam_sb[:], lam.rearrange("(p t) -> p t", t=PACK))
         b_raw = staged("b_raw", [P, PACK, N], F32, B_AT)
         nc.sync.dma_start(b_raw[:], b.rearrange("(p j) n -> p j n", j=PACK))
         bias_sb = staged("bias_sb", [P, N // P], F32, BIAS_AT)

@@ -29,8 +29,8 @@ def tile_list_adapter_moderation_probs_kernel(tc, tab, offs, w0_words, w0_scales
         keep = ctx.enter_context(tc.tile_pool(name="keep", bufs=1))
         psum = ctx.enter_context(tc.psum_pool(name="psum", bufs=1))
 
-        def sb(name, shape, dtype, align=64):
-            return keep.tile(shape, dtype, name=name, align_bytes=align)
+        def sb(name, shape, dtype):
+            return keep.tile(shape, dtype, name=name, align_bytes=256)
 
         offsets = sb("offsets", [P, S // 16], U16)
 
@@ -92,7 +92,7 @@ def tile_list_adapter_moderation_probs_kernel(tc, tab, offs, w0_words, w0_scales
         w0_sb = sb("w0_sb", [P, PASSES, 2 * N], U8)
         nc.sync.dma_start(w0_sb[:].bitcast(I32), w0_words.rearrange("a p c -> p a c").bitcast(I32))
 
-        a_bf = [sb(f"a_bf{g}", [P, PACK, P, PACK], BF16, 256) for g in range(PASSES)]
+        a_bf = [sb(f"a_bf{g}", [P, PACK, P, PACK], BF16) for g in range(PASSES)]
         a_codes, a_plane = {}, {}
 
         def cast_rows(g, raw, lo_j, hi_j):

@@ -37,14 +37,12 @@ def tile_list_adapter_moderation_probs_kernel(tc, tab, offs, w0_words, w0_scales
         stage = ctx.enter_context(tc.tile_pool(name="stage", bufs=1))
         KB = 1024
         WORDS_AT = [0, 16 * KB]
-        SCALE_WIN_AT = WORDS_AT[1]
+        SCALE_WIN_AT = 84 * KB
         A_RAW_AT = {0: 34 * KB, 1: 42 * KB, 2: 50 * KB, 3: 58 * KB}
-        PICKED_SCALES_AT = A_RAW_AT[0]
-        PICKED_AT = {(0, 0): 49 * KB, (0, 1): 61 * KB, (1, 0): 70 * KB, (1, 1): 70 * KB}
-        STACKED_AT = 78 * KB
-        LAM_AT = 70 * KB
-        BIAS_AT = 70 * KB + 256
-        B_AT = 71 * KB
+        PICKED_AT = {(0, 0): 41 * KB, (0, 1): 57 * KB, (1, 0): 65 * KB + 512, (1, 1): 65 * KB + 512}
+        LAM_AT = 66 * KB
+        BIAS_AT = 66 * KB + 256
+        B_AT = 67 * KB
 
         def staged(name, shape, dtype, at):
             return stage.tile(shape, dtype, name=name, align_bytes=256, offset=at)
@@ -52,7 +50,7 @@ def tile_list_adapter_moderation_probs_kernel(tc, tab, offs, w0_words, w0_scales
         scale_win = staged("scale_win", [P, T // 4], I32, SCALE_WIN_AT)
         for m in range(2):
             nc.sync.dma_start(
-                scale_win[32 + 32 * m : 64 + 32 * m, :], tab[m, 512 * T :].rearrange("(q t) -> q t", t=T).bitcast(I32)
+                scale_win[32 + m : 96 : 2, :], tab[m, 512 * T :].rearrange("(h q t) -> q h t", h=2, t=T).bitcast(I32)
             )
             if m == 0:
                 nc.sync.dma_start(offsets[:], offs)
@@ -60,9 +58,8 @@ def tile_list_adapter_moderation_probs_kernel(tc, tab, offs, w0_words, w0_scales
         nc.vector.memset(scale_win[96:P, :], 0)
         w0_plane = sb("w0_plane", [P, PASSES, N], U8)
         nc.gpsimd.memset(w0_plane[:].rearrange("p a n -> p (a n)").bitcast(I32), 0)
-        planes = [sb(f"v_plane{h}", [P, 2, S], U8) for h in range(2)]
-        for h in range(2):
-            nc.gpsimd.memset(planes[h][:].rearrange("p m s -> p (m s)").bitcast(I32), 0)
+        planes = sb("v_planes", [P, PASSES, S], U8)
+        nc.gpsimd.memset(planes[:].rearrange("p a s -> p (a s)").bitcast(I32), 0)
         for r in range(4):
             nc.gpsimd.dma_start(
                 w0_plane[r : P : 32, :, :].bitcast(I32),
@@ -101,10 +98,7 @@ def tile_list_adapter_moderation_probs_kernel(tc, tab, offs, w0_words, w0_scales
                 copy(a_bf[g][:, lo : lo + 2, :, lo_j:hi_j].rearrange("p t m j -> p m j t"), src[:, :, :, lo : lo + 2])
 
         def quant_a(g, parts):
-            if g == 0:
-                a_codes[g] = staged("a_codes0", [P, R], U32, STACKED_AT)
-            else:
-                a_codes[g] = sb(f"a_codes{g}", [P, R], U32)
+            a_codes[g] = sb(f"a_codes{g}", [P, R], U32)
             a_plane[g] = sb(f"a_plane{g}", [P, R], U8)
             flat = a_bf[g][:].rearrange("p t m j -> p (t m j)")
             w = R // parts
@@ -152,27 +146,18 @@ def tile_list_adapter_moderation_probs_kernel(tc, tab, offs, w0_words, w0_scales
             for hf, t in early:
                 down(g, hf, t)
 
-        picked_scales = staged("picked_scales", [P, S], U8, PICKED_SCALES_AT)
+        picked_scales = sb("picked_scales", [P, S], U8)
         nc.vector.tensor_copy(picked_scales[:], scale_win[:].bitcast(U8).indirect(offsets[:]))
-        stacked = staged("stacked", [P, 2, S // 4], I32, STACKED_AT)
-        nc.sync.dma_start(stacked[32:64, 1, :], picked_scales[64:96, :].bitcast(I32))
-        nc.vector.tensor_copy(stacked[32:64, 0, :], picked_scales[32:64, :].bitcast(I32))
         load_words(1)
-
-        def move_planes(h):
-            for r in range(4):
-                first = 32 + 16 * h + r
-                nc.sync.dma_start(
-                    planes[h][r : P : 32, :, :].rearrange("p m s -> p (m s)").bitcast(I32),
-                    stacked[first : first + 13 : 4, :, :].rearrange("p m s -> p (m s)"),
-                )
-
-        v_plane = {g: planes[g % 2][:, g // 2, :] for g in range(PASSES)}
-        move_planes(0)
-        load_a(0)
-        move_planes(1)
+        for q in (0, 2, 1, 3):
+            nc.sync.dma_start(
+                planes[32 * q : 32 * q + 4, :, :].bitcast(I32),
+                picked_scales[32 + 16 * q : 48 + 16 * q, :].bitcast(I32),
+            )
+        v_plane = {g: planes[:, 2 * (g % 2) + g // 2, :] for g in range(PASSES)}
         gather_words(0)
-        for g in range(1, PASSES):
+        gather_words(1)
+        for g in range(PASSES):
             load_a(g)
 
         h_codes, h_plane = [], []
@@ -231,7 +216,6 @@ def tile_list_adapter_moderation_probs_kernel(tc, tab, offs, w0_words, w0_scales
             nc.scalar.activation(prob[:], acc[:, : hi - lo], ACT.Sigmoid, bias=bias_sb[:, u : u + 1])
             nc.sync.dma_start(out[P * u : P * (u + 1), lo:hi], prob[:])
 
-        gather_words(1)
         lam_sb = staged("lam_sb", [P, PACK], F32, LAM_AT)
         nc.sync.dma_start(lam_sb[:], lam.rearrange("(p t) -> p t", t=PACK))
         b_raw = staged("b_raw", [P, PACK, N], F32, B_AT)
@@ -241,7 +225,7 @@ def tile_list_adapter_moderation_probs_kernel(tc, tab, offs, w0_words, w0_scales
             nc.sync.dma_start(bias_sb[:], bias.rearrange("(u p) -> p u", p=P))
 
         y_first = [bank(f"y_first{u}", 6 + u) for u in range(2)]
-        for g in (0, 2, 1, 3):
+        for g in range(PASSES):
             for u in range(2):
                 base(y_first[u], u, 0, HALF, (g,))
         for g in range(PASSES - 1):

@@ -21,6 +21,7 @@ PACK = 4
 PASSES = K // (P * PACK)
 HALF = 512
 HALVES = S // HALF
+PIECE = 256
 
 
 def tile_list_adapter_moderation_probs_kernel(tc, tab, offs, w0_words, w0_scales, a, b, lam, bias, out):
@@ -38,8 +39,9 @@ def tile_list_adapter_moderation_probs_kernel(tc, tab, offs, w0_words, w0_scales
         KB = 1024
         WORDS_AT = [0, 16 * KB]
         SCALE_WIN_AT = 84 * KB
-        A_RAW_AT = {0: 34 * KB, 1: 42 * KB, 2: 50 * KB, 3: 58 * KB}
-        PICKED_AT = {(0, 0): 41 * KB, (0, 1): 57 * KB, (1, 0): 65 * KB + 512, (1, 1): 65 * KB + 512}
+        A_RAW_AT = {0: 0, 1: 8 * KB, 2: 50 * KB, 3: 58 * KB}
+        PICKED_AT = {(0, 0): 57 * KB, (0, 1): 40 * KB, (1, 0): 65 * KB + 512, (1, 1): 42 * KB}
+        PARTED_AT = 72 * KB
         LAM_AT = 66 * KB
         BIAS_AT = 66 * KB + 256
         B_AT = 67 * KB
@@ -112,13 +114,16 @@ def tile_list_adapter_moderation_probs_kernel(tc, tab, offs, w0_words, w0_scales
         v_words = {}
 
         def gather_words(m):
+            picked = []
             for hf in range(HALVES):
-                g = staged(f"picked{m}_{hf}", [P, HALF], I32, PICKED_AT[m, hf])
+                picked.append(staged(f"picked{m}_{hf}", [P, HALF], I32, PICKED_AT[m, hf]))
                 nc.vector.tensor_copy(
-                    g[:].bitcast(U32), words_win[m][:].bitcast(U32).indirect(offsets[:, 32 * hf : 32 * (hf + 1)])
+                    picked[hf][:].bitcast(U32),
+                    words_win[m][:].bitcast(U32).indirect(offsets[:, 32 * hf : 32 * (hf + 1)]),
                 )
-                parted = sb(f"parted{m}_{hf}", [P, 2, HALF], U16)
-                nc.vector.tensor_copy(parted[:], g[:].bitcast(U16).rearrange("p (n h) -> p h n", h=2))
+            for hf in range(HALVES):
+                parted = staged(f"parted{m}_{hf}", [P, 2, HALF], U16, PARTED_AT + 2 * KB * (2 * m + hf))
+                nc.vector.tensor_copy(parted[:], picked[hf][:].bitcast(U16).rearrange("p (n h) -> p h n", h=2))
                 for h in range(2):
                     v_words[2 * m + h, hf] = parted[:, h, :]
 
@@ -131,20 +136,21 @@ def tile_list_adapter_moderation_probs_kernel(tc, tab, offs, w0_words, w0_scales
         for i, (hf, t) in enumerate(early):
             h_acc[hf, t] = bank(f"h_acc{hf}_{t}", i)
 
-        def down(g, hf, t):
+        def down(acc, g, t, lo, hi):
+            hf, c = divmod(lo, HALF)
             nc.tensor.matmul_mx(
-                out=h_acc[hf, t][:],
+                out=acc[:, : hi - lo],
                 lhsT=a_codes[g][:, P * t : P * (t + 1)].bitcast(FP8X4),
                 lhsT_scale=a_plane[g][:, P * t : P * (t + 1)],
-                rhs=v_words[g, hf].bitcast(FP4X4),
-                rhs_scale=v_plane[g][:, HALF * hf : HALF * (hf + 1)],
+                rhs=v_words[g, hf][:, c : c + hi - lo].bitcast(FP4X4),
+                rhs_scale=v_plane[g][:, lo:hi],
                 start=(g == 0),
                 stop=(g == PASSES - 1),
             )
 
         def down_pass(g):
             for hf, t in early:
-                down(g, hf, t)
+                down(h_acc[hf, t], g, t, HALF * hf, HALF * (hf + 1))
 
         picked_scales = sb("picked_scales", [P, S], U8)
         nc.vector.tensor_copy(picked_scales[:], scale_win[:].bitcast(U8).indirect(offsets[:]))
@@ -168,27 +174,26 @@ def tile_list_adapter_moderation_probs_kernel(tc, tab, offs, w0_words, w0_scales
             h_codes.append(sb(f"h_codes{hf}", [P, HALF], U32))
             h_plane.append(sb(f"h_plane{hf}", [P, HALF], U8))
 
-        def evac_h(hf, t, on_vector):
+        def evac_h(acc, hf, t, lo, hi, on_vector=False):
             if on_vector:
-                nc.vector.tensor_scalar(h_rows[hf][:, t, :], h_acc[hf, t][:], lam_sb[:, t : t + 1], None, op0=MULT)
+                nc.vector.tensor_scalar(h_rows[hf][:, t, lo:hi], acc, lam_sb[:, t : t + 1], None, op0=MULT)
             else:
-                nc.scalar.activation(h_rows[hf][:, t, :], h_acc[hf, t][:], ACT.Copy, scale=lam_sb[:, t : t + 1])
+                nc.scalar.activation(h_rows[hf][:, t, lo:hi], acc, ACT.Copy, scale=lam_sb[:, t : t + 1])
 
-        def quant_h(hf, lo, hi):
+        def weave_h(hf, lo, hi):
             nc.vector.tensor_copy(
                 h_mix[hf][:, lo:hi, :].rearrange("p (c i) t -> p c t i", i=4),
                 h_rows[hf][:, :, lo:hi].rearrange("p t (c i) -> p c t i", i=4),
             )
+
+        def quant_h(hf, lo, hi):
             nc.vector.quantize_mx(
                 out=h_codes[hf][:, lo:hi].bitcast(FP8X4),
                 scales=h_plane[hf][:, lo:hi],
                 in_=h_mix[hf][:, lo:hi, :].rearrange("p n t -> p (n t)"),
             )
 
-        b_codes = sb("b_codes", [P, N], U32)
-        b_plane = sb("b_plane", [P, N], U8)
-
-        def base(acc, u, lo, hi, passes):
+        def base(acc, u, lo, hi, passes, closes=False):
             hf, c = divmod(lo, HALF)
             for g in passes:
                 nc.tensor.matmul_mx(
@@ -197,11 +202,11 @@ def tile_list_adapter_moderation_probs_kernel(tc, tab, offs, w0_words, w0_scales
                     lhsT_scale=w0_plane[:, g, P * u : P * (u + 1)],
                     rhs=v_words[g, hf][:, c : c + hi - lo].bitcast(FP4X4),
                     rhs_scale=v_plane[g][:, lo:hi],
-                    start=(g == 0),
-                    stop=False,
+                    start=(g == 0 and not closes),
+                    stop=(g == PASSES - 1 and closes),
                 )
 
-        def up(acc, u, lo, hi):
+        def up(acc, u, lo, hi, opens=False):
             hf, c = divmod(lo, HALF)
             nc.tensor.matmul_mx(
                 out=acc[:, : hi - lo],
@@ -209,9 +214,11 @@ def tile_list_adapter_moderation_probs_kernel(tc, tab, offs, w0_words, w0_scales
                 lhsT_scale=b_plane[:, P * u : P * (u + 1)],
                 rhs=h_codes[hf][:, c : c + hi - lo].bitcast(FP8X4),
                 rhs_scale=h_plane[hf][:, c : c + hi - lo],
-                start=False,
-                stop=True,
+                start=opens,
+                stop=not opens,
             )
+
+        def finish(acc, u, lo, hi):
             prob = sb(f"prob{u}_{lo}", [P, hi - lo], F32)
             nc.scalar.activation(prob[:], acc[:, : hi - lo], ACT.Sigmoid, bias=bias_sb[:, u : u + 1])
             nc.sync.dma_start(out[P * u : P * (u + 1), lo:hi], prob[:])
@@ -241,25 +248,37 @@ def tile_list_adapter_moderation_probs_kernel(tc, tab, offs, w0_words, w0_scales
         nc.vector.tensor_copy(
             b_bf[:].rearrange("p (c i) j -> p c j i", i=4), b_raw[:].rearrange("p j (c i) -> p c j i", i=4)
         )
+        for t in range(PACK):
+            evac_h(h_acc[0, t][:], 0, t, 0, HALF, on_vector=(t == 3))
+        b_codes = staged("b_codes", [P, N], U32, PARTED_AT + 4 * KB)
+        b_plane = sb("b_plane", [P, N], U8)
         nc.vector.quantize_mx(
             out=b_codes[:].bitcast(FP8X4), scales=b_plane[:], in_=b_bf[:].rearrange("p n j -> p (n j)")
         )
-        for t in range(PACK):
-            evac_h(0, t, t == 3)
-        quant_h(0, 0, HALF)
+        for step in (weave_h, quant_h):
+            for lo in (0, PIECE):
+                step(0, lo, lo + PIECE)
         for t in range(2):
-            evac_h(1, t, False)
-        for t in range(2, PACK):
-            h_acc[1, t] = bank(f"h_acc1_{t}", t - 2)
-            for g in range(PASSES):
-                down(g, 1, t)
-            evac_h(1, t, False)
+            evac_h(h_acc[1, t][:], 1, t, 0, HALF)
+        for c in range(2):
+            for t in range(2, PACK):
+                acc = bank(f"h_late{c}_{t}", 2 * c + t - 2)
+                for g in range(PASSES):
+                    down(acc, g, t, HALF + PIECE * c, HALF + PIECE * (c + 1))
+                evac_h(acc[:, :PIECE], 1, t, PIECE * c, PIECE * (c + 1))
         for u in range(2):
             up(y_first[u], u, 0, HALF)
-        for c in range(2):
-            lo = HALF + 256 * c
-            quant_h(1, 256 * c, 256 * (c + 1))
-            y_rest = [bank(f"y_rest{c}_{u}", 2 + 2 * c + u) for u in range(2)]
-            for u in range(2):
-                base(y_rest[u], u, lo, lo + 256, range(PASSES))
-                up(y_rest[u], u, lo, lo + 256)
+            finish(y_first[u], u, 0, HALF)
+        for step in (weave_h, quant_h):
+            for lo in (0, PIECE):
+                step(1, lo, lo + PIECE)
+        y_rest = {(c, u): bank(f"y_rest{c}_{u}", (4 + 2 * c + u) % 6) for c in range(2) for u in range(2)}
+        for c, u in y_rest:
+            lo = HALF + PIECE * c
+            last = (c, u) == (1, 1)
+            if last:
+                up(y_rest[c, u], u, lo, lo + PIECE, opens=True)
+            base(y_rest[c, u], u, lo, lo + PIECE, range(PASSES), closes=last)
+            if not last:
+                up(y_rest[c, u], u, lo, lo + PIECE)
+            finish(y_rest[c, u], u, lo, lo + PIECE)

@@ -60,7 +60,7 @@ def tile_list_adapter_moderation_probs_kernel(tc, tab, offs, w0_words, w0_scales
         nc.vector.memset(scale_win[96:P, :], 0)
         w0_plane = sb("w0_plane", [P, PASSES, N], U8)
         nc.gpsimd.memset(w0_plane[:].rearrange("p a n -> p (a n)").bitcast(I32), 0)
-        planes = sb("v_planes", [P, PASSES, S], U8)
+        planes = sb("v_planes", [P, PASSES, S - PIECE], U8)
         nc.gpsimd.memset(planes[:].rearrange("p a s -> p (a s)").bitcast(I32), 0)
         for r in range(4):
             nc.gpsimd.dma_start(
@@ -132,35 +132,44 @@ def tile_list_adapter_moderation_probs_kernel(tc, tab, offs, w0_words, w0_scales
         def bank(name, i):
             return psum.tile([P, HALF], F32, name=name, tag=f"bank{i}")
 
-        early = [(0, 0), (0, 1), (0, 2), (0, 3), (1, 0), (1, 1)]
-        for i, (hf, t) in enumerate(early):
-            h_acc[hf, t] = bank(f"h_acc{hf}_{t}", i)
+        for t in range(PACK):
+            h_acc[t] = bank(f"h_acc{t}", t)
+        h_pair = bank("h_pair", 4)
 
-        def down(acc, g, t, lo, hi):
+        def down(acc, g, t, lo, hi, opens=True, closes=True):
             hf, c = divmod(lo, HALF)
             nc.tensor.matmul_mx(
                 out=acc[:, : hi - lo],
                 lhsT=a_codes[g][:, P * t : P * (t + 1)].bitcast(FP8X4),
                 lhsT_scale=a_plane[g][:, P * t : P * (t + 1)],
                 rhs=v_words[g, hf][:, c : c + hi - lo].bitcast(FP4X4),
-                rhs_scale=v_plane[g][:, lo:hi],
-                start=(g == 0),
-                stop=(g == PASSES - 1),
+                rhs_scale=v_plane(g, lo, hi),
+                start=(g == 0 and opens),
+                stop=(g == PASSES - 1 and closes),
             )
 
         def down_pass(g):
-            for hf, t in early:
-                down(h_acc[hf, t], g, t, HALF * hf, HALF * (hf + 1))
+            for t in range(PACK):
+                down(h_acc[t], g, t, 0, HALF)
+            for t in range(2):
+                down(h_pair[:, PIECE * t : PIECE * (t + 1)], g, t, HALF, HALF + PIECE, opens=(t == 0), closes=(t == 1))
 
         picked_scales = sb("picked_scales", [P, S], U8)
         nc.vector.tensor_copy(picked_scales[:], scale_win[:].bitcast(U8).indirect(offsets[:]))
         load_words(1)
-        for q in (0, 2, 1, 3):
-            nc.sync.dma_start(
-                planes[32 * q : 32 * q + 4, :, :].bitcast(I32),
-                picked_scales[32 + 16 * q : 48 + 16 * q, :].bitcast(I32),
-            )
-        v_plane = {g: planes[:, 2 * (g % 2) + g // 2, :] for g in range(PASSES)}
+
+        def move_planes(dst, lo, hi):
+            for q in (0, 2, 1, 3):
+                nc.sync.dma_start(
+                    dst[32 * q : 32 * q + 4, :, :].bitcast(I32),
+                    picked_scales[32 + 16 * q : 48 + 16 * q, lo:hi].bitcast(I32),
+                )
+
+        def v_plane(g, lo, hi):
+            c = 2 * (g % 2) + g // 2
+            return planes[:, c, lo:hi] if hi <= S - PIECE else last_planes[:, c, lo - (S - PIECE) : hi - (S - PIECE)]
+
+        move_planes(planes, 0, S - PIECE)
         gather_words(0)
         gather_words(1)
         for g in range(PASSES):
@@ -193,7 +202,7 @@ def tile_list_adapter_moderation_probs_kernel(tc, tab, offs, w0_words, w0_scales
                 in_=h_mix[hf][:, lo:hi, :].rearrange("p n t -> p (n t)"),
             )
 
-        def base(acc, u, lo, hi, passes, closes=False):
+        def base(acc, u, lo, hi, passes, opens=True, closes=False):
             hf, c = divmod(lo, HALF)
             for g in passes:
                 nc.tensor.matmul_mx(
@@ -201,12 +210,12 @@ def tile_list_adapter_moderation_probs_kernel(tc, tab, offs, w0_words, w0_scales
                     lhsT=w0_sb[:, g, 2 * P * u : 2 * P * (u + 1)].bitcast(FP4X4),
                     lhsT_scale=w0_plane[:, g, P * u : P * (u + 1)],
                     rhs=v_words[g, hf][:, c : c + hi - lo].bitcast(FP4X4),
-                    rhs_scale=v_plane[g][:, lo:hi],
-                    start=(g == 0 and not closes),
+                    rhs_scale=v_plane(g, lo, hi),
+                    start=(g == 0 and opens),
                     stop=(g == PASSES - 1 and closes),
                 )
 
-        def up(acc, u, lo, hi, opens=False):
+        def up(acc, u, lo, hi, opens=False, closes=True):
             hf, c = divmod(lo, HALF)
             nc.tensor.matmul_mx(
                 out=acc[:, : hi - lo],
@@ -215,7 +224,7 @@ def tile_list_adapter_moderation_probs_kernel(tc, tab, offs, w0_words, w0_scales
                 rhs=h_codes[hf][:, c : c + hi - lo].bitcast(FP8X4),
                 rhs_scale=h_plane[hf][:, c : c + hi - lo],
                 start=opens,
-                stop=not opens,
+                stop=closes,
             )
 
         def finish(acc, u, lo, hi):
@@ -230,11 +239,16 @@ def tile_list_adapter_moderation_probs_kernel(tc, tab, offs, w0_words, w0_scales
         bias_sb = staged("bias_sb", [P, N // P], F32, BIAS_AT)
         with nc.allow_non_contiguous_dma(reason="one bias value a partition"):
             nc.sync.dma_start(bias_sb[:], bias.rearrange("(u p) -> p u", p=P))
+        last_planes = staged("v_last_planes", [P, PASSES, PIECE], U8, PICKED_AT[1, 1])
+        move_planes(last_planes, S - PIECE, S)
 
         y_first = [bank(f"y_first{u}", 6 + u) for u in range(2)]
+        y_pair = bank("y_pair", 5)
         for g in range(PASSES):
             for u in range(2):
                 base(y_first[u], u, 0, HALF, (g,))
+            for u in range(2):
+                base(y_pair[:, PIECE * u : PIECE * (u + 1)], u, HALF, HALF + PIECE, (g,), opens=(u == 0))
         for g in range(PASSES - 1):
             cast_rows(g, a_raw[g], 0, PACK)
             quant_a(g, 2)
@@ -249,7 +263,7 @@ def tile_list_adapter_moderation_probs_kernel(tc, tab, offs, w0_words, w0_scales
             b_bf[:].rearrange("p (c i) j -> p c j i", i=4), b_raw[:].rearrange("p j (c i) -> p c j i", i=4)
         )
         for t in range(PACK):
-            evac_h(h_acc[0, t][:], 0, t, 0, HALF, on_vector=(t == 3))
+            evac_h(h_acc[t][:], 0, t, 0, HALF, on_vector=(t == 3))
         b_codes = staged("b_codes", [P, N], U32, PARTED_AT + 4 * KB)
         b_plane = sb("b_plane", [P, N], U8)
         nc.vector.quantize_mx(
@@ -259,26 +273,25 @@ def tile_list_adapter_moderation_probs_kernel(tc, tab, offs, w0_words, w0_scales
             for lo in (0, PIECE):
                 step(0, lo, lo + PIECE)
         for t in range(2):
-            evac_h(h_acc[1, t][:], 1, t, 0, HALF)
-        for c in range(2):
-            for t in range(2, PACK):
-                acc = bank(f"h_late{c}_{t}", 2 * c + t - 2)
-                for g in range(PASSES):
-                    down(acc, g, t, HALF + PIECE * c, HALF + PIECE * (c + 1))
-                evac_h(acc[:, :PIECE], 1, t, PIECE * c, PIECE * (c + 1))
+            evac_h(h_pair[:, PIECE * t : PIECE * (t + 1)], 1, t, 0, PIECE)
+        late = [(0, 2), (0, 3), (1, 0), (1, 1), (1, 2), (1, 3)]
+        for i, (c, t) in enumerate(late):
+            acc = bank(f"h_late{c}_{t}", (0, 1, 3, 2, 4, 0)[i])
+            for g in range(PASSES):
+                down(acc, g, t, HALF + PIECE * c, HALF + PIECE * (c + 1))
+            evac_h(acc[:, :PIECE], 1, t, PIECE * c, PIECE * (c + 1))
         for u in range(2):
             up(y_first[u], u, 0, HALF)
             finish(y_first[u], u, 0, HALF)
-        for step in (weave_h, quant_h):
-            for lo in (0, PIECE):
-                step(1, lo, lo + PIECE)
-        y_rest = {(c, u): bank(f"y_rest{c}_{u}", (4 + 2 * c + u) % 6) for c in range(2) for u in range(2)}
-        for c, u in y_rest:
-            lo = HALF + PIECE * c
-            last = (c, u) == (1, 1)
-            if last:
-                up(y_rest[c, u], u, lo, lo + PIECE, opens=True)
-            base(y_rest[c, u], u, lo, lo + PIECE, range(PASSES), closes=last)
-            if not last:
-                up(y_rest[c, u], u, lo, lo + PIECE)
-            finish(y_rest[c, u], u, lo, lo + PIECE)
+        for lo in (0, PIECE):
+            weave_h(1, lo, lo + PIECE)
+            quant_h(1, lo, lo + PIECE)
+        for u in range(2):
+            up(y_pair[:, PIECE * u : PIECE * (u + 1)], u, HALF, HALF + PIECE, closes=(u == 1))
+        for u in range(2):
+            finish(y_pair[:, PIECE * u : PIECE * (u + 1)], u, HALF, HALF + PIECE)
+        for u in range(2):
+            y_last = bank(f"y_last{u}", (1, 3)[u])
+            base(y_last, u, S - PIECE, S, range(PASSES))
+            up(y_last, u, S - PIECE, S)
+            finish(y_last, u, S - PIECE, S)

@@ -103,13 +103,14 @@ def tile_list_adapter_moderation_probs_kernel(tc, tab, offs, w0_words, w0_scales
             a_codes[g] = sb(f"a_codes{g}", [P, R], U32)
             a_plane[g] = sb(f"a_plane{g}", [P, R], U8)
             flat = a_bf[g][:].rearrange("p t m j -> p (t m j)")
-            w = R // parts
-            for i in range(parts):
+            lo = 0
+            for w in parts:
                 nc.vector.quantize_mx(
-                    out=a_codes[g][:, i * w : (i + 1) * w].bitcast(FP8X4),
-                    scales=a_plane[g][:, i * w : (i + 1) * w],
-                    in_=flat[:, 4 * i * w : 4 * (i + 1) * w],
+                    out=a_codes[g][:, lo : lo + w].bitcast(FP8X4),
+                    scales=a_plane[g][:, lo : lo + w],
+                    in_=flat[:, 4 * lo : 4 * (lo + w)],
                 )
+                lo = lo + w
 
         v_words = {}
 
@@ -251,11 +252,16 @@ def tile_list_adapter_moderation_probs_kernel(tc, tab, offs, w0_words, w0_scales
                 base(y_pair[:, PIECE * u : PIECE * (u + 1)], u, HALF, HALF + PIECE, (g,), opens=(u == 0))
         for g in range(PASSES - 1):
             cast_rows(g, a_raw[g], 0, PACK)
-            quant_a(g, 2)
+            quant_a(g, (2 * P, 2 * P))
             down_pass(g)
-        for e in range(2):
-            cast_rows(3, a_raw[3, e], 2 * e, 2 * e + 2)
-        quant_a(3, 4)
+        cast_rows(3, a_raw[3, 0], 0, 2)
+        src = a_raw[3, 1][:].rearrange("p j (m t) -> p m j t", t=PACK)
+        for lo in (0, P // 2):
+            nc.vector.tensor_copy(
+                a_bf[3][:, 0:2, lo : lo + P // 2, 2:4].rearrange("p t m j -> p m j t"), src[:, lo : lo + P // 2, :, 0:2]
+            )
+        nc.scalar.copy(a_bf[3][:, 2:4, :, 2:4].rearrange("p t m j -> p m j t"), src[:, :, :, 2:4])
+        quant_a(3, (P // 2, P // 2, P, P, P))
         down_pass(3)
 
         b_bf = sb("b_bf", [P, N, PACK], BF16)
@@ -283,9 +289,10 @@ def tile_list_adapter_moderation_probs_kernel(tc, tab, offs, w0_words, w0_scales
         for u in range(2):
             up(y_first[u], u, 0, HALF)
             finish(y_first[u], u, 0, HALF)
-        for lo in (0, PIECE):
-            weave_h(1, lo, lo + PIECE)
-            quant_h(1, lo, lo + PIECE)
+        for piece in (0, PIECE):
+            for step in (weave_h, quant_h):
+                for lo in (piece, piece + P):
+                    step(1, lo, lo + P)
         for u in range(2):
             up(y_pair[:, PIECE * u : PIECE * (u + 1)], u, HALF, HALF + PIECE, closes=(u == 1))
         for u in range(2):

@@ -59,9 +59,7 @@ def tile_list_adapter_moderation_probs_kernel(tc, tab, offs, w0_words, w0_scales
         nc.vector.memset(scale_win[0:32, :], 0)
         nc.vector.memset(scale_win[96:P, :], 0)
         w0_plane = sb("w0_plane", [P, PASSES, N], U8)
-        nc.gpsimd.memset(w0_plane[:].rearrange("p a n -> p (a n)").bitcast(I32), 0)
         planes = sb("v_planes", [P, PASSES, S - PIECE], U8)
-        nc.gpsimd.memset(planes[:].rearrange("p a s -> p (a s)").bitcast(I32), 0)
         for r in range(4):
             nc.gpsimd.dma_start(
                 w0_plane[r : P : 32, :, :].bitcast(I32),

@@ -61,7 +61,7 @@ def tile_list_adapter_moderation_probs_kernel(tc, tab, offs, w0_words, w0_scales
         w0_plane = sb("w0_plane", [P, PASSES, N], U8)
         planes = sb("v_planes", [P, PASSES, S - PIECE], U8)
         for r in range(4):
-            nc.gpsimd.dma_start(
+            nc.scalar.dma_start(
                 w0_plane[r : P : 32, :, :].bitcast(I32),
                 w0_scales.rearrange("a (q r) n -> r q a n", r=4)[r].bitcast(I32),
             )
@@ -86,6 +86,7 @@ def tile_list_adapter_moderation_probs_kernel(tc, tab, offs, w0_words, w0_scales
             nc.sync.dma_start(words_win[m][:], tab[m, : 512 * T].rearrange("(p c) -> p c", p=P).bitcast(I32))
 
         load_words(0)
+        load_words(1)
         w0_sb = sb("w0_sb", [P, PASSES, 2 * N], U8)
         nc.sync.dma_start(w0_sb[:].bitcast(I32), w0_words.rearrange("a p c -> p a c").bitcast(I32))
 
@@ -94,7 +95,8 @@ def tile_list_adapter_moderation_probs_kernel(tc, tab, offs, w0_words, w0_scales
 
         def cast_rows(g, raw, lo_j, hi_j):
             src = raw[:].rearrange("p j (m t) -> p m j t", t=PACK)
-            for lo, copy in ((0, nc.scalar.copy if g == 0 else nc.vector.tensor_copy), (2, nc.scalar.copy)):
+            first, second = (nc.scalar.copy, nc.vector.tensor_copy) if g == 0 else (nc.vector.tensor_copy, nc.scalar.copy)
+            for lo, copy in ((0, first), (2, second)):
                 copy(a_bf[g][:, lo : lo + 2, :, lo_j:hi_j].rearrange("p t m j -> p m j t"), src[:, :, :, lo : lo + 2])
 
         def quant_a(g, parts):
@@ -155,11 +157,10 @@ def tile_list_adapter_moderation_probs_kernel(tc, tab, offs, w0_words, w0_scales
 
         picked_scales = sb("picked_scales", [P, S], U8)
         nc.vector.tensor_copy(picked_scales[:], scale_win[:].bitcast(U8).indirect(offsets[:]))
-        load_words(1)
 
-        def move_planes(dst, lo, hi):
+        def move_planes(dst, lo, hi, queue):
             for q in (0, 2, 1, 3):
-                nc.sync.dma_start(
+                queue.dma_start(
                     dst[32 * q : 32 * q + 4, :, :].bitcast(I32),
                     picked_scales[32 + 16 * q : 48 + 16 * q, lo:hi].bitcast(I32),
                 )
@@ -168,7 +169,7 @@ def tile_list_adapter_moderation_probs_kernel(tc, tab, offs, w0_words, w0_scales
             c = 2 * (g % 2) + g // 2
             return planes[:, c, lo:hi] if hi <= S - PIECE else last_planes[:, c, lo - (S - PIECE) : hi - (S - PIECE)]
 
-        move_planes(planes, 0, S - PIECE)
+        move_planes(planes, 0, S - PIECE, nc.scalar)
         gather_words(0)
         gather_words(1)
         for g in range(PASSES):
@@ -239,7 +240,7 @@ def tile_list_adapter_moderation_probs_kernel(tc, tab, offs, w0_words, w0_scales
         with nc.allow_non_contiguous_dma(reason="one bias value a partition"):
             nc.sync.dma_start(bias_sb[:], bias.rearrange("(u p) -> p u", p=P))
         last_planes = staged("v_last_planes", [P, PASSES, PIECE], U8, PICKED_AT[1, 1])
-        move_planes(last_planes, S - PIECE, S)
+        move_planes(last_planes, S - PIECE, S, nc.sync)
 
         y_first = [bank(f"y_first{u}", 6 + u) for u in range(2)]
         y_pair = bank("y_pair", 5)

@@ -95,9 +95,18 @@ def tile_list_adapter_moderation_probs_kernel(tc, tab, offs, w0_words, w0_scales
 
         def cast_rows(g, raw, lo_j, hi_j):
             src = raw[:].rearrange("p j (m t) -> p m j t", t=PACK)
-            first, second = (nc.scalar.copy, nc.vector.tensor_copy) if g == 0 else (nc.vector.tensor_copy, nc.scalar.copy)
-            for lo, copy in ((0, first), (2, second)):
-                copy(a_bf[g][:, lo : lo + 2, :, lo_j:hi_j].rearrange("p t m j -> p m j t"), src[:, :, :, lo : lo + 2])
+            vector, scalar = nc.vector.tensor_copy, nc.scalar.copy
+            if g == 0:
+                cuts = ((scalar, 0, 0, P), (vector, 2, 0, P // 2), (scalar, 2, P // 2, P))
+            elif g < PASSES - 1:
+                cuts = ((vector, 0, 0, P // 2), (vector, 0, P // 2, P), (scalar, 2, 0, P))
+            else:
+                cuts = ((vector, 0, 0, P), (scalar, 2, 0, P))
+            for copy, t, lo, hi in cuts:
+                copy(
+                    a_bf[g][:, t : t + 2, lo:hi, lo_j:hi_j].rearrange("p t m j -> p m j t"),
+                    src[:, lo:hi, :, t : t + 2],
+                )
 
         def quant_a(g, parts):
             a_codes[g] = sb(f"a_codes{g}", [P, R], U32)
@@ -251,7 +260,7 @@ def tile_list_adapter_moderation_probs_kernel(tc, tab, offs, w0_words, w0_scales
                 base(y_pair[:, PIECE * u : PIECE * (u + 1)], u, HALF, HALF + PIECE, (g,), opens=(u == 0))
         for g in range(PASSES - 1):
             cast_rows(g, a_raw[g], 0, PACK)
-            quant_a(g, (2 * P, 2 * P))
+            quant_a(g, (2 * P, 2 * P) if g == 0 else (P // 2, P // 2, P, 2 * P))
             down_pass(g)
         cast_rows(3, a_raw[3, 0], 0, 2)
         src = a_raw[3, 1][:].rearrange("p j (m t) -> p m j t", t=PACK)

@@ -161,8 +161,10 @@ def tile_list_adapter_moderation_probs_kernel(tc, tab, offs, w0_words, w0_scales
         def down_pass(g):
             for t in range(PACK):
                 down(h_acc[t], g, t, 0, HALF)
-            for t in range(2):
-                down(h_pair[:, PIECE * t : PIECE * (t + 1)], g, t, HALF, HALF + PIECE, opens=(t == 0), closes=(t == 1))
+                if t < 2:
+                    down(
+                        h_pair[:, PIECE * t : PIECE * (t + 1)], g, t, HALF, HALF + PIECE, opens=(t == 0), closes=(t == 1)
+                    )
 
         picked_scales = sb("picked_scales", [P, S], U8)
         nc.vector.tensor_copy(picked_scales[:], scale_win[:].bitcast(U8).indirect(offsets[:]))

from contextlib import ExitStack

import concourse.mybir as mybir

K, R, N, T, S = 2048, 512, 256, 4096, 1024
FLOPS = 2 * S * (K * R + K * N + R * N)

F32 = mybir.dt.float32
BF16 = mybir.dt.bfloat16
I32 = mybir.dt.int32
U32 = mybir.dt.uint32
U16 = mybir.dt.uint16
U8 = mybir.dt.uint8
FP8X4 = mybir.dt.float8_e4m3fn_x4
FP4X4 = mybir.dt.float4_e2m1fn_x4
ACT = mybir.ActivationFunctionType
MULT = mybir.AluOpType.mult

P = 128
PACK = 4
PASSES = K // (P * PACK)
HALF = 512
HALVES = S // HALF
PIECE = 256


def tile_list_adapter_moderation_probs_kernel(tc, tab, offs, w0_words, w0_scales, a, b, lam, bias, out):
    nc = tc.nc
    with ExitStack() as ctx:
        keep = ctx.enter_context(tc.tile_pool(name="keep", bufs=1))
        psum = ctx.enter_context(tc.psum_pool(name="psum", bufs=1))

        def sb(name, shape, dtype):
            return keep.tile(shape, dtype, name=name, align_bytes=256)

        offsets = sb("offsets", [P, S // 16], U16)

        stage = ctx.enter_context(tc.tile_pool(name="stage", bufs=1))
        KB = 1024
        WORDS_AT = [0, 16 * KB]
        SCALE_WIN_AT = 84 * KB
        A_RAW_AT = {0: 0, 1: 8 * KB, 2: 50 * KB, 3: 58 * KB}
        PICKED_AT = {(0, 0): 57 * KB, (0, 1): 40 * KB, (1, 0): 65 * KB + 512, (1, 1): 42 * KB}
        PARTED_AT = 72 * KB
        LAM_AT = 66 * KB
        BIAS_AT = 66 * KB + 256
        B_AT = 67 * KB

        def staged(name, shape, dtype, at):
            return stage.tile(shape, dtype, name=name, align_bytes=256, offset=at)

        scale_win = staged("scale_win", [P, T // 4], I32, SCALE_WIN_AT)
        for m in range(2):
            nc.sync.dma_start(
                scale_win[32 + m : 96 : 2, :], tab[m, 512 * T :].rearrange("(h q t) -> q h t", h=2, t=T).bitcast(I32)
            )
            if m == 0:
                nc.sync.dma_start(offsets[:], offs)
        nc.vector.memset(scale_win[0:32, :], 0)
        nc.vector.memset(scale_win[96:P, :], 0)
        w0_plane = sb("w0_plane", [P, PASSES, N], U8)
        planes = sb("v_planes", [P, PASSES, S - PIECE], U8)
        for r in range(4):
            nc.scalar.dma_start(
                w0_plane[r : P : 32, :, :].bitcast(I32),
                w0_scales.rearrange("a (q r) n -> r q a n", r=4)[r].bitcast(I32),
            )
        warm = sb("warm", [P, 2], F32)
        nc.vector.memset(warm[:, 0:1], 0.0)
        nc.scalar.activation(warm[:, 1:2], warm[:, 0:1], ACT.Sigmoid)

        a_raw, words_win = {}, {}

        def load_a(g):
            rows = a[512 * g : 512 * (g + 1), :].rearrange("(p j) r -> p j r", j=PACK)
            if g < PASSES - 1:
                a_raw[g] = staged(f"a_raw{g}", [P, PACK, R], F32, A_RAW_AT[g])
                nc.sync.dma_start(a_raw[g][:], rows)
                return
            for e in range(2):
                a_raw[g, e] = staged(f"a_raw{g}_{e}", [P, 2, R], F32, A_RAW_AT[g] + 4 * KB * e)
                nc.sync.dma_start(a_raw[g, e][:], rows[:, 2 * e : 2 * e + 2, :])

        def load_words(m):
            words_win[m] = staged(f"words_win{m}", [P, T], I32, WORDS_AT[m])
            nc.sync.dma_start(words_win[m][:], tab[m, : 512 * T].rearrange("(p c) -> p c", p=P).bitcast(I32))

        load_words(0)
        load_words(1)
        w0_sb = sb("w0_sb", [P, PASSES, 2 * N], U8)
        nc.sync.dma_start(w0_sb[:].bitcast(I32), w0_words.rearrange("a p c -> p a c").bitcast(I32))

        a_bf = [sb(f"a_bf{g}", [P, PACK, P, PACK], BF16) for g in range(PASSES)]
        a_codes, a_plane = {}, {}

        def cast_rows(g, raw, lo_j, hi_j):
            src = raw[:].rearrange("p j (m t) -> p m j t", t=PACK)
            vector, scalar = nc.vector.tensor_copy, nc.scalar.copy
            if g == 0:
                cuts = ((scalar, 0, 0, P), (vector, 2, 0, P // 2), (scalar, 2, P // 2, P))
            elif g < PASSES - 1:
                cuts = ((vector, 0, 0, P // 2), (vector, 0, P // 2, P), (scalar, 2, 0, P))
            else:
                cuts = ((vector, 0, 0, P), (scalar, 2, 0, P))
            for copy, t, lo, hi in cuts:
                copy(
                    a_bf[g][:, t : t + 2, lo:hi, lo_j:hi_j].rearrange("p t m j -> p m j t"),
                    src[:, lo:hi, :, t : t + 2],
                )

        def quant_a(g, parts):
            a_codes[g] = sb(f"a_codes{g}", [P, R], U32)
            a_plane[g] = sb(f"a_plane{g}", [P, R], U8)
            flat = a_bf[g][:].rearrange("p t m j -> p (t m j)")
            lo = 0
            for w in parts:
                nc.vector.quantize_mx(
                    out=a_codes[g][:, lo : lo + w].bitcast(FP8X4),
                    scales=a_plane[g][:, lo : lo + w],
                    in_=flat[:, 4 * lo : 4 * (lo + w)],
                )
                lo = lo + w

        v_words = {}

        def gather_words(m):
            picked = []
            for hf in range(HALVES):
                picked.append(staged(f"picked{m}_{hf}", [P, HALF], I32, PICKED_AT[m, hf]))
                nc.vector.tensor_copy(
                    picked[hf][:].bitcast(U32),
                    words_win[m][:].bitcast(U32).indirect(offsets[:, 32 * hf : 32 * (hf + 1)]),
                )
            for hf in range(HALVES):
                parted = staged(f"parted{m}_{hf}", [P, 2, HALF], U16, PARTED_AT + 2 * KB * (2 * m + hf))
                nc.vector.tensor_copy(parted[:], picked[hf][:].bitcast(U16).rearrange("p (n h) -> p h n", h=2))
                for h in range(2):
                    v_words[2 * m + h, hf] = parted[:, h, :]

        h_acc = {}

        def bank(name, i):
            return psum.tile([P, HALF], F32, name=name, tag=f"bank{i}")

        for t in range(PACK):
            h_acc[t] = bank(f"h_acc{t}", t)
        h_pair = bank("h_pair", 4)

        def down(acc, g, t, lo, hi, opens=True, closes=True):
            hf, c = divmod(lo, HALF)
            nc.tensor.matmul_mx(
                out=acc[:, : hi - lo],
                lhsT=a_codes[g][:, P * t : P * (t + 1)].bitcast(FP8X4),
                lhsT_scale=a_plane[g][:, P * t : P * (t + 1)],
                rhs=v_words[g, hf][:, c : c + hi - lo].bitcast(FP4X4),
                rhs_scale=v_plane(g, lo, hi),
                start=(g == 0 and opens),
                stop=(g == PASSES - 1 and closes),
            )

        def down_pass(g):
            for t in range(PACK):
                down(h_acc[t], g, t, 0, HALF)
                if t < 2:
                    down(
                        h_pair[:, PIECE * t : PIECE * (t + 1)], g, t, HALF, HALF + PIECE, opens=(t == 0), closes=(t == 1)
                    )

        picked_scales = sb("picked_scales", [P, S], U8)
        nc.vector.tensor_copy(picked_scales[:], scale_win[:].bitcast(U8).indirect(offsets[:]))

        def move_planes(dst, lo, hi, queue):
            for q in (0, 2, 1, 3):
                queue.dma_start(
                    dst[32 * q : 32 * q + 4, :, :].bitcast(I32),
                    picked_scales[32 + 16 * q : 48 + 16 * q, lo:hi].bitcast(I32),
                )

        def v_plane(g, lo, hi):
            c = 2 * (g % 2) + g // 2
            return planes[:, c, lo:hi] if hi <= S - PIECE else last_planes[:, c, lo - (S - PIECE) : hi - (S - PIECE)]

        move_planes(planes, 0, S - PIECE, nc.scalar)
        gather_words(0)
        gather_words(1)
        for g in range(PASSES):
            load_a(g)

        h_codes, h_plane = [], []
        h_rows, h_mix = [], []
        for hf in range(HALVES):
            h_rows.append(sb(f"h_rows{hf}", [P, PACK, HALF], BF16))
            h_mix.append(sb(f"h_mix{hf}", [P, HALF, PACK], BF16))
            h_codes.append(sb(f"h_codes{hf}", [P, HALF], U32))
            h_plane.append(sb(f"h_plane{hf}", [P, HALF], U8))

        def evac_h(acc, hf, t, lo, hi, on_vector=False):
            if on_vector:
                nc.vector.tensor_scalar(h_rows[hf][:, t, lo:hi], acc, lam_sb[:, t : t + 1], None, op0=MULT)
            else:
                nc.scalar.activation(h_rows[hf][:, t, lo:hi], acc, ACT.Copy, scale=lam_sb[:, t : t + 1])

        def weave_h(hf, lo, hi):
            nc.vector.tensor_copy(
                h_mix[hf][:, lo:hi, :].rearrange("p (c i) t -> p c t i", i=4),
                h_rows[hf][:, :, lo:hi].rearrange("p t (c i) -> p c t i", i=4),
            )

        def quant_h(hf, lo, hi):
            nc.vector.quantize_mx(
                out=h_codes[hf][:, lo:hi].bitcast(FP8X4),
                scales=h_plane[hf][:, lo:hi],
                in_=h_mix[hf][:, lo:hi, :].rearrange("p n t -> p (n t)"),
            )

        def base(acc, u, lo, hi, passes, opens=True, closes=False):
            hf, c = divmod(lo, HALF)
            for g in passes:
                nc.tensor.matmul_mx(
                    out=acc[:, : hi - lo],
                    lhsT=w0_sb[:, g, 2 * P * u : 2 * P * (u + 1)].bitcast(FP4X4),
                    lhsT_scale=w0_plane[:, g, P * u : P * (u + 1)],
                    rhs=v_words[g, hf][:, c : c + hi - lo].bitcast(FP4X4),
                    rhs_scale=v_plane(g, lo, hi),
                    start=(g == 0 and opens),
                    stop=(g == PASSES - 1 and closes),
                )

        def up(acc, u, lo, hi, opens=False, closes=True):
            hf, c = divmod(lo, HALF)
            nc.tensor.matmul_mx(
                out=acc[:, : hi - lo],
                lhsT=b_codes[:, P * u : P * (u + 1)].bitcast(FP8X4),
                lhsT_scale=b_plane[:, P * u : P * (u + 1)],
                rhs=h_codes[hf][:, c : c + hi - lo].bitcast(FP8X4),
                rhs_scale=h_plane[hf][:, c : c + hi - lo],
                start=opens,
                stop=closes,
            )

        def finish(acc, u, lo, hi):
            prob = sb(f"prob{u}_{lo}", [P, hi - lo], F32)
            nc.scalar.activation(prob[:], acc[:, : hi - lo], ACT.Sigmoid, bias=bias_sb[:, u : u + 1])
            nc.sync.dma_start(out[P * u : P * (u + 1), lo:hi], prob[:])

        lam_sb = staged("lam_sb", [P, PACK], F32, LAM_AT)
        nc.sync.dma_start(lam_sb[:], lam.rearrange("(p t) -> p t", t=PACK))
        b_raw = staged("b_raw", [P, PACK, N], F32, B_AT)
        nc.sync.dma_start(b_raw[:], b.rearrange("(p j) n -> p j n", j=PACK))
        bias_sb = staged("bias_sb", [P, N // P], F32, BIAS_AT)
        with nc.allow_non_contiguous_dma(reason="one bias value a partition"):
            nc.sync.dma_start(bias_sb[:], bias.rearrange("(u p) -> p u", p=P))
        last_planes = staged("v_last_planes", [P, PASSES, PIECE], U8, PICKED_AT[1, 1])
        move_planes(last_planes, S - PIECE, S, nc.sync)

        y_first = [bank(f"y_first{u}", 6 + u) for u in range(2)]
        y_pair = bank("y_pair", 5)
        for g in range(PASSES):
            for u in range(2):
                base(y_first[u], u, 0, HALF, (g,))
            for u in range(2):
                base(y_pair[:, PIECE * u : PIECE * (u + 1)], u, HALF, HALF + PIECE, (g,), opens=(u == 0))
        for g in range(PASSES - 1):
            cast_rows(g, a_raw[g], 0, PACK)
            quant_a(g, (2 * P, 2 * P) if g == 0 else (P // 2, P // 2, P, 2 * P))
            down_pass(g)
        cast_rows(3, a_raw[3, 0], 0, 2)
        src = a_raw[3, 1][:].rearrange("p j (m t) -> p m j t", t=PACK)
        for lo in (0, P // 2):
            nc.vector.tensor_copy(
                a_bf[3][:, 0:2, lo : lo + P // 2, 2:4].rearrange("p t m j -> p m j t"), src[:, lo : lo + P // 2, :, 0:2]
            )
        nc.scalar.copy(a_bf[3][:, 2:4, :, 2:4].rearrange("p t m j -> p m j t"), src[:, :, :, 2:4])
        quant_a(3, (P // 2, P // 2, P, P, P))
        down_pass(3)

        b_bf = sb("b_bf", [P, N, PACK], BF16)
        nc.vector.tensor_copy(
            b_bf[:].rearrange("p (c i) j -> p c j i", i=4), b_raw[:].rearrange("p j (c i) -> p c j i", i=4)
        )
        for t in range(PACK):
            evac_h(h_acc[t][:], 0, t, 0, HALF, on_vector=(t == 3))
        b_codes = staged("b_codes", [P, N], U32, PARTED_AT + 4 * KB)
        b_plane = sb("b_plane", [P, N], U8)
        nc.vector.quantize_mx(
            out=b_codes[:].bitcast(FP8X4), scales=b_plane[:], in_=b_bf[:].rearrange("p n j -> p (n j)")
        )
        for step in (weave_h, quant_h):
            for lo in (0, PIECE):
                step(0, lo, lo + PIECE)
        for t in range(2):
            evac_h(h_pair[:, PIECE * t : PIECE * (t + 1)], 1, t, 0, PIECE)
        late = [(0, 2), (0, 3), (1, 0), (1, 1), (1, 2), (1, 3)]
        for i, (c, t) in enumerate(late):
            acc = bank(f"h_late{c}_{t}", (0, 1, 3, 2, 4, 0)[i])
            for g in range(PASSES):
                down(acc, g, t, HALF + PIECE * c, HALF + PIECE * (c + 1))
            evac_h(acc[:, :PIECE], 1, t, PIECE * c, PIECE * (c + 1))
        for u in range(2):
            up(y_first[u], u, 0, HALF)
            finish(y_first[u], u, 0, HALF)
        for piece in (0, PIECE):
            for step in (weave_h, quant_h):
                for lo in (piece, piece + P):
                    step(1, lo, lo + P)
        for u in range(2):
            up(y_pair[:, PIECE * u : PIECE * (u + 1)], u, HALF, HALF + PIECE, closes=(u == 1))
        for u in range(2):
            finish(y_pair[:, PIECE * u : PIECE * (u + 1)], u, HALF, HALF + PIECE)
        for u in range(2):
            y_last = bank(f"y_last{u}", (1, 3)[u])
            base(y_last, u, S - PIECE, S, range(PASSES))
            up(y_last, u, S - PIECE, S)
            finish(y_last, u, S - PIECE, S)
